import numpy as np, ml_dtypes
CORES = [6,15,38,47]
N = 4
BF = ml_dtypes.bfloat16
def gentries(a):
    return np.ascontiguousarray(a.reshape(8, 16, -1).transpose(0, 2, 1)).reshape(8, -1)
def gtable(e):
    e = np.asarray(e); return np.ascontiguousarray(e.reshape(8, -1, 16).transpose(0, 2, 1)).reshape(128, -1).astype(np.int32)
W, K, NM, SM, RO = 4096, 4096, 4095, 31, 6
def walks(rng):
    pace = rng.choice(np.array([0.02, 0.1, 0.4, 1.0]), (N, 8, 16, 1))
    x = rng.integers(-3, 4, (N, 8, 16, W)) * (rng.random((N, 8, 16, W), dtype=np.float32) < pace)
    x[..., 0] = rng.integers(-SM, SM + 1, (N, 8, 16))
    return np.abs((np.add.accumulate(x, axis=-1) + SM) % (4 * SM) - 2 * SM) - SM
def spans(rng):
    u = np.exp2(6 + rng.random((8, K)) * (np.log2(NM + 1) - 6)).astype(np.int64)
    return np.clip(np.where(rng.random((8, K)) < 0.5, u, rng.integers(64, NM + 1, (8, K))), 64, NM)
def starts(rng, n, power=1):
    return np.minimum((rng.random((N, 8, K)) ** power * (W - n)).astype(np.int64), W - 1 - n)
def pack(s, lo, n):
    return {"walk": np.ascontiguousarray(s.reshape(N, 128, W)).astype(np.float32).astype(BF), "lo": np.stack([gtable(a) for a in lo]), "span": np.stack([gtable(n)] * N)}
def setup_inputs(rng):
    s = walks(rng); n = spans(rng)
    return pack(s, starts(rng, n), n)
def setup_inputs_ends(rng):
    s = walks(rng); n = rng.choice(np.array([64, 65, 127, 128, NM - 1, NM]), (8, K)); lo = starts(rng, n)
    k = rng.integers(0, 3, (N, 8, K)); lo = np.where(k == 0, 0, np.where(k == 1, W - 1 - n, lo))
    s[:, 0] = SM; s[:, 0, :, 0] = -SM; s[:, 0, :, NM] = -SM; s[:, 0, ::2] = -s[:, 0, ::2]
    n[0, ::2] = NM; lo[:, 0, ::2] = 0; n[0, 1::2] = 64; lo[:, 0, 1::2] = np.minimum(lo[:, 0, 1::2], W - 65)
    s[:, 1] = SM * (2 * rng.integers(0, 2, (N, 16, W)) - 1)
    n[3] = NM; lo[:, 3] = rng.integers(0, W - NM, (N, 1))
    s[:, 2] = SM - rng.integers(0, 2, (N, 16, W))
    s[:, 2, :, :32] *= -1; s[:, 2, :, NM - 31:NM + 1] *= -1
    s[:, 2] *= 2 * rng.integers(0, 2, (N, 16, 1)) - 1
    n[2] = NM - rng.integers(0, 32, K); lo[:, 2] = np.minimum((rng.random((N, K)) * (NM - n[2] + 1)).astype(np.int64), NM - n[2])
    h = NM >> 2; q = int(rng.integers(0, N)); j = int(rng.integers(0, 16)); i = rng.integers(0, 16, N)
    s[:, 4] = SM
    s[q, 4, j] = SM - 1; s[q, 4, j, h - 15:h + 5] = SM - 2; s[q, 4, j, 3 * h - 45:3 * h + 6] = SM
    s[:, 4, :, :4] = -SM; s[:, 4, :, 4 * h - 60:NM + 1] = -SM
    for a in range(N): s[a, 4, int(i[a]), 4 * h - 60:NM + 1] = 1 - SM
    s[:, 4] *= 2 * rng.integers(0, 2, (N, 16, 1)) - 1
    n[4] = 4 * (h - rng.integers(0, 16, K)) + rng.choice(np.array([0, 1, 3]), K); n[4, :3] = 4 * h + np.array([1, 0, 3])
    lo[:, 4] = np.minimum(rng.integers(0, 4, (N, K)), NM - n[4])
    c = rng.integers(-SM, SM + 1, (N, 2, 16)); e = rng.integers(1, SM + 1, (N, 2, 16)); e = np.where(c > 0, c - e, c + e)
    last = rng.integers(NM, W, N); begin = rng.integers(0, W - NM, N); more = spans(rng)
    for a in range(N):
        s[a, 5] = c[a, 0][:, None]; s[a, 5, :, int(last[a])] = e[a, 0]
        s[a, 6] = c[a, 1][:, None]; s[a, 6, :, int(begin[a])] = e[a, 1]
    n[5] = np.where(rng.random(K) < 0.5, NM - rng.integers(0, 63, K), more[5]); n[5, 0] = NM - 30; lo[:, 5] = last[:, None] - n[5]
    n[6] = np.where(rng.random(K) < 0.5, 1024 + 2 * rng.integers(0, 100, K), more[6]); n[6, 0] = 1024; lo[:, 6] = begin[:, None]
    return pack(s, lo, n)
def setup_inputs_ties(rng):
    amp = rng.integers(1, SM + 1, (N, 8, 16, 1)) * (2 * rng.integers(0, 2, (N, 8, 16, 1)) - 1)
    pat = np.repeat(rng.integers(0, 2, (N, 8, 1, W // 64)), 64, axis=-1); n = spans(rng); lo = starts(rng, n)
    pat[:, 1::2] = pat[:1, 1::2].copy(); lo[:, 1::2] = lo[:1, 1::2].copy(); pat[:, 6] = 1
    return pack(amp * pat, lo, n)
def setup_inputs_short(rng):
    s = walks(rng); n = rng.integers(64, 97, (8, K)); lo = starts(rng, n)
    u = np.arange(W) % 64; saw = np.where(u == 0, -SM, SM - (u * SM >> 5)); v = (64 - u) % 64; was = np.where(v == 0, -SM, SM - (v * SM >> 5))
    sg = 2 * rng.integers(0, 2, (N, 16, 1)) - 1
    s[:, 0] = sg * saw; s[:, 4] = sg * was; s[:, 2, ::2] = saw; s[:, 6, 1::2] = was
    n[::2] = 64; lo[:, ::2] = 64 * rng.integers(0, W // 64 - 1, (N, 4, K))
    tail = np.maximum(-SM, SM - 64 + np.arange(66)); tail[0] = -SM; tail[65] = -SM
    s[:, 1, :, W - 66:] = sg * tail; n[1, ::4] = 65; lo[:, 1, ::4] = W - 66
    return pack(s, lo, n)
def setup_inputs_uneven(rng):
    s = walks(rng); n = spans(rng); lo = starts(rng, n); big = rng.integers(0, N, 8); big[0] = 0; big[1] = N - 1
    keep = np.arange(N)[:, None] == big[None, :]
    s = np.where(keep[:, :, None, None], s, np.sign(s))
    one = s[big[5], 5, 3].copy(); s[:, 5] = 0; s[big[5], 5, 3] = one
    k = rng.integers(0, 5, K); n[7] = n[7][k]; lo[:, 7] = lo[:, 7][:, k]
    return pack(s, lo, n)
def setup_inputs_spread(rng):
    z = np.exp2(-rng.integers(0, 6, (N, 8, 1, W)).astype(np.float64)) * (rng.random((N, 8, 1, W)) > 0.0625)
    s = np.rint(SM * z * (2 * rng.random((N, 8, 16, W)) - 1)).astype(np.int64); n = spans(rng)
    return pack(s, starts(rng, n, 4), n)
def check_inputs(d):
    bad = []; s = d["walk"].astype(np.float32); lo = d["lo"].astype(np.int64); n = d["span"].astype(np.int64)
    if not np.all((np.abs(s) <= SM) & (s == np.rint(s))): bad.append("whole numbers of walk")
    if np.min(n) < 64 or np.max(n) > NM: bad.append("range of span")
    if not np.all(n == n[:1]): bad.append("span alike on all ranks")
    if np.min(lo) < 0 or np.max(lo + n) > W - 1: bad.append("range of lo")
    return bad
def reference(walk, lo, span):
    s = walk.astype(np.float32).astype(np.int64).reshape(N, 8, 16, W)
    at = np.stack([gentries(a) for a in lo]).astype(np.int64)
    n = gentries(span[0]).astype(np.int64)
    def pick(q, t):
        return np.take_along_axis(s[q], (at[q] + t)[:, None, :], 2)
    first = [pick(q, 0 * n) for q in range(N)]; rise = [pick(q, n) - first[q] for q in range(N)]
    def gain(t):
        g = np.zeros((8, K), np.int64)
        for q in range(N):
            g = g + np.add.reduce(np.abs(n[:, None, :] * (pick(q, t) - first[q]) - t[:, None, :] * rise[q]), axis=1)
        return g
    l = np.zeros((8, K), np.int64); r = n.copy(); m = n >> 1; gm = gain(m)
    for rnd in range(RO):
        a = r - m; b = m - l; right = a > b
        w = np.where(right, m + (a >> 1), m - (b >> 1))
        gw = gain(w); up = gw > gm
        end = np.where(up, m, w); low = right == up
        l = np.where(low, end, l); r = np.where(low, r, end)
        m = np.where(up, w, m); gm = np.where(up, gw, gm)
    return {"ym": np.stack([gtable(m)] * N).astype(np.float32), "yg": np.stack([gtable(gm)] * N).astype(np.float32)}

@@ -1,0 +1,587 @@
+from concourse.bass import DstId, RemoteDMATransfer
+from concourse.mybir import AluOpType, ActivationFunctionType
+
+ALU = AluOpType
+ACT = ActivationFunctionType
+N = 4
+RO = 6
+C0 = 2048.0
+OFF = 0
+SPLIT = False
+PLACE = {'p1': -0.677, 'sb0': -2.356, 'tb0': -4.084, 'sb1': -0.146, 'tb1': -2.441, 'v1a': 0.232, 'g10': 0.361,
+         'g11': 0.518, 'v2b': 0.234, 'l10': -2.037, 'l11': 0.239, 'dec': 0.265, 'lis': 0.455, 'v3a': 0.34,
+         'pu0': -3.317, 'pu1': -2.806, 'sa0': 0.614, 'gx0': 0.67, 'gx1': 0.859, 'v1b': 0.976, 'px': 0.546,
+         'ta0': -2.262, 'lx0': -0.518, 'lx1': 0.081, 'lat': 1.978, 'v2x': 1.195, 'sa1': 0.978, 'ta1': 1.029,
+         'v3b': 0.995}
+
+SCRATCH = {
+    "wst": ("dram", [6, 128, 512], "bfloat16"),
+    "wld": ("dram", [6, 128, 512], "bfloat16"),
+    "lst": ("dram", [4, 128, 64], "int32"),
+    "lld": ("dram", [3, 128, 64], "int32"),
+    "res": ("sbuf", [128, 2, 4, 16], "float32"),
+    "rld": ("sbuf", [128, 6, 4, 16], "float32"),
+    "win": ("sbuf", [128, 4096], "bfloat16"),
+    "xg": ("sbuf", [128, 4096], "bfloat16"),
+    "s0": ("sbuf", [128, 4096], "bfloat16"),
+    "rise": ("sbuf", [128, 4096], "bfloat16"),
+    "nb": ("sbuf", [128, 4096], "float32"),
+    "yy": ("sbuf", [128, 3072], "float32"),
+    "uu": ("sbuf", [128, 2048], "float32"),
+    "dd": ("sbuf", [128, 2048], "float32"),
+    "jj": ("sbuf", [128, 128], "bfloat16"),
+    "kk": ("sbuf", [128, 128], "bfloat16"),
+    "kt": ("sbuf", [128, 128], "bfloat16"),
+    "pcol": ("sbuf", [128, 4], "int32"),
+    "pbit": ("sbuf", [128, 4], "int32"),
+    "pflt": ("sbuf", [128, 4], "float32"),
+    "srow": ("sbuf", [128, 4], "float32"),
+    "ind": ("sbuf", [128, 4], "float32"),
+    "idb": ("sbuf", [128, 128], "bfloat16"),
+    "nid": ("sbuf", [128, 128], "bfloat16"),
+    "idh": ("sbuf", [128, 128], "float16"),
+    "selo": ("sbuf", [128, 16, 128], "float16"),
+    "selt": ("sbuf", [128, 16, 128], "float16"),
+    "zero": ("sbuf", [128, 256], "float16"),
+    "n32": ("sbuf", [128, 2, 32], "int32"),
+    "lo32": ("sbuf", [128, 256], "int32"),
+    "loc": ("sbuf", [128, 256], "float16"),
+    "log": ("sbuf", [128, 256], "float16"),
+    "off": ("sbuf", [128, 9 * 256], "uint16"),
+    "t2": ("sbuf", [128, 16, 128], "float16"),
+    "nn": ("sbuf", [128, 2, 32], "int32"),
+    "tmp": ("sbuf", [128, 4, 32], "int32"),
+    "st": ("sbuf", [128, 48, 32], "int32"),
+    "pk": ("sbuf", [128, 16, 64], "float32"),
+    "sg": ("sbuf", [128, 16, 32], "float32"),
+    "up": ("sbuf", [128, 16, 64], "float32"),
+    "dl": ("sbuf", [128, 16, 64], "float32"),
+    "gm": ("sbuf", [128, 16, 64], "float32"),
+    "tau": ("sbuf", [128, 16, 32], "float32"),
+    "dx": ("sbuf", [128, 16, 32], "float32"),
+    "qq": ("sbuf", [128, 16, 32], "float32"),
+    "mu": ("sbuf", [128, 2, 32], "float32"),
+    "w16": ("sbuf", [128, 16, 40], "float16"),
+    "pa": ("psum", [128, 1024], "float32"),
+    "pb0": ("psum", [128, 1024], "float32"),
+    "pb1": ("psum", [128, 1024], "float32"),
+    "pg": ("psum", [128, 512], "float32"),
+    "po": ("psum", [128, 512], "float32"),
+}
+SEMAPHORES = (["cv", "ca", "cp", "cg", "sent", "lstg", "wstg0", "wstg1", "larr", "nld", "lold", "winld", "outs"]
+              + ["warr%d" % k for k in range(6)] + ["rarr%d" % k for k in range(3)] + ["acc%d" % k for k in range(4)])
+
+PSUM_KEYS = ("pa0", "pa1", "pb00", "pb01", "pb10", "pb11", "pg", "po")
+
+
+def rank_program(g, core, T, topo):
+    r = T.rank_of(core)
+    if r is None:
+        return
+    Q = {"v": g.vector, "a": g.scalar, "p": g.tensor, "g": g, "s": g.sync}
+    plan = []
+    place = [(-9, "dec")]
+
+    def op(q, call, reads, writes, sem=None, total=0, fresh=False, pre=()):
+        plan.append(dict(q=q, call=call, reads=reads, writes=writes, sem=sem, total=total, fresh=fresh, pre=pre,
+                         at=place[0]))
+
+    def arrange():
+        n = len(plan)
+        before = [set() for _ in range(n)]
+        wr, rd, last = {}, {}, {}
+        for i, o in enumerate(plan):
+            for k in o["reads"]:
+                before[i].update(wr.get(k, ()))
+                if k in PSUM_KEYS:
+                    before[i].update(j for j in rd.get(k, ()) if plan[j]["q"] != o["q"])
+            if not o["fresh"]:
+                for k in o["writes"]:
+                    before[i].update(wr.get(k, ()))
+                    before[i].update(rd.get(k, ()))
+            if o["q"] in "gs" or o["sem"] is not None:
+                if o["q"] in last:
+                    before[i].add(~last[o["q"]])
+                last[o["q"]] = i
+            for k in o["reads"]:
+                rd.setdefault(k, []).append(i)
+            for k in o["writes"]:
+                if o["fresh"]:
+                    wr.setdefault(k, []).append(i)
+                else:
+                    wr[k] = [i]
+                    rd[k] = []
+            before[i].discard(i)
+        after = [[] for _ in range(n)]
+        left = [0] * n
+        for i in range(n):
+            for j in set(j if j >= 0 else ~j for j in before[i]):
+                after[j].append(i)
+                left[i] += 1
+        rank = [(o["at"][0] + PLACE[o["at"][1]], i) for i, o in enumerate(plan)]
+        ready = [rank[i] for i in range(n) if left[i] == 0]
+        out = []
+        while ready:
+            ready.sort()
+            i = ready.pop(0)[1]
+            out.append(i)
+            for j in after[i]:
+                left[j] -= 1
+                if left[j] == 0:
+                    ready.append(rank[j])
+        return out
+
+    cnt = {"v": 0, "a": 0, "p": 0, "g": 0}
+    seen = {q: {} for q in Q}
+    writer, readers, totals = {}, {}, {}
+
+    def wait(q, sem, val):
+        if seen[q].get(sem, 0) < val:
+            Q[q].wait_ge(T.sem[sem], val)
+            seen[q][sem] = val
+
+    def emit(o):
+        q = o["q"]
+        own = "c" + q
+        need = dict(o["pre"])
+
+        def add(mark):
+            if mark is not None and not (q == "p" and mark[0] == own):
+                need[mark[0]] = max(need.get(mark[0], 0), mark[1])
+        for k in o["reads"]:
+            add(writer.get(k))
+            if k in PSUM_KEYS:
+                for s, v in readers.get(k, {}).items():
+                    if s != own:
+                        add((s, v))
+        if not o["fresh"]:
+            for k in o["writes"]:
+                add(writer.get(k))
+                for s, v in readers.get(k, {}).items():
+                    add((s, v))
+        for s in sorted(need):
+            wait(q, s, need[s])
+        made = o["call"]()
+        if o["sem"] == "":
+            return
+        if o["sem"] is None:
+            made.then_inc(T.sem[own], 1)
+            cnt[q] += 1
+            mark = (own, cnt[q])
+        else:
+            made.then_inc(T.sem[o["sem"]], 16)
+            totals[o["sem"]] = o["total"]
+            mark = (o["sem"], o["total"])
+        if not o["fresh"]:
+            for k in o["reads"]:
+                readers.setdefault(k, {})[mark[0]] = mark[1]
+        for k in o["writes"]:
+            writer[k] = mark
+            readers[k] = {}
+
+    def dma(q, out, in_, reads, writes, sem, total, pre=()):
+        op(q, lambda: Q[q].dma_start(out, in_), reads, writes, sem, total, True, pre)
+
+    def tt(out, a, b, alu, reads, writes):
+        op("v", lambda: g.vector.tensor_tensor(out, a, b, alu), reads, writes)
+
+    def ts(out, a, s1, s2, o0, o1, reads, writes):
+        if o1 is None:
+            op("v", lambda: g.vector.tensor_scalar(out, a, s1, None, o0), reads, writes)
+        else:
+            op("v", lambda: g.vector.tensor_scalar(out, a, s1, s2, o0, o1), reads, writes)
+
+    def cp(out, a, reads, writes):
+        op("v", lambda: g.vector.tensor_copy(out, a), reads, writes)
+
+    def mm(out, lhsT, rhs, start, stop, reads, writes):
+        op("p", lambda: g.tensor.matmul(out, lhsT, rhs, start, stop), reads, writes)
+
+    def act(out, a, func, reads, writes):
+        op("a", lambda: g.scalar.activation(out, a, func), reads, writes)
+
+    sent = [0]
+
+    def send(parts, reads):
+        trs = []
+        for x, e0, ne, src, dst, sem in parts:
+            peer = T.cores[r ^ x]
+            rid, pid, _ = topo.addr(peer)
+            mask = 0
+            for e in topo.engines(core, peer)[e0:e0 + ne]:
+                mask |= 1 << e
+            trs.append(RemoteDMATransfer(dst_ids=[DstId(rid=rid, pnc=pid)], dma_engine_mask=mask,
+                                         remote_sem=T.sem[sem], src=src, dst=dst))
+            sent[0] += ne
+        op("g", lambda: g.remote_dma_fused(trs, local_sem=T.sem.sent), reads, [], "")
+
+    peers = (3, 1, 2)
+    deal = (((0, 4), (4, 2), (6, 2)), ((0, 2), (4, 4), (2, 2)))
+
+    dma("s", T.lst[:], T.lo[:], [], ["lst"], "lstg", 16)
+    for s in range(2):
+        for i, x in enumerate(peers):
+            row = 32 * (r ^ x) + 16 * s
+            dma("s" if (s == 0) == (i != 2) else "a", T.wst[3 * s + i], T.walk[row:row + 16, :], [], ["wst%d" % s],
+                "wstg%d" % s, 48)
+    for s in range(2):
+        row = 32 * r + 16 * s
+        dma("a", T.n32[:, s, :], T.span[row:row + 16, :], [], ["n32"], "nld", 32)
+    dma("s", T.win[32 * r:32 * r + 32, :], T.walk[32 * r:32 * r + 32, :], [], ["win"], "winld", 112)
+    for s in range(2):
+        row = 32 * r + 16 * s
+        c = (2 * r + s) * 32
+        dma("a", T.lo32[:, c:c + 32], T.lo[row:row + 16, :], [], ["lo32"], "lold", 128)
+
+    op("g", lambda: g.iota(T.jj[:], [[1, 128]], 0, -1, allow_small_or_imprecise_dtypes=True), [], ["jj"])
+    op("g", lambda: g.iota(T.kt[:], [[0, 4], [16, 2], [0, 16]], 0, -1, allow_small_or_imprecise_dtypes=True), [], ["kt"])
+    op("g", lambda: g.iota(T.kk[:], [[0, 4], [128, 2], [1, 16]], 0, -1, allow_small_or_imprecise_dtypes=True), [], ["kk"])
+    op("g", lambda: g.iota(T.pcol[:], [[0, 4]], 0, 1), [], ["pcol"])
+    op("g", lambda: g.iota(T.srow[:], [[0, 2], [1, 2]], 0, 0, allow_small_or_imprecise_dtypes=True), [], ["srow"])
+
+    send([(x, deal[0][i][0], deal[0][i][1], T.lst[r ^ x], T.lld[i], "larr") for i, x in enumerate(peers)], ["lst"])
+    for s in range(2):
+        send([(x, deal[s][i][0], deal[s][i][1], T.wst[3 * s + i], T.wld[3 * s + i], "warr%d" % (3 * s + i))
+              for i, x in enumerate(peers)], ["wst%d" % s])
+
+    op("v", lambda: g.vector.memset(T.w16[:, :, 32:33], C0), [], ["w16c"])
+    op("v", lambda: g.vector.memset(T.zero[:], 0.0), [], ["zero"])
+    ts(T.idb[:], T.jj[:], 0.0, None, ALU.is_equal, None, ["jj"], ["idb"])
+    ts(T.idh[:], T.jj[:], 0.0, None, ALU.is_equal, None, ["jj"], ["idh"])
+    ts(T.nid[:], T.jj[:], 0.0, -1.0, ALU.is_equal, ALU.mult, ["jj"], ["nid"])
+    for c in range(16):
+        ts(T.selt[0:33, c, :], T.kt[0:33, :], float(-c), T.idb[0:33, 32:33], ALU.is_equal, ALU.max, ["kt", "idb"], ["selt%d" % c])
+
+    def sti(k, b):
+        return (2 * k + b) * 3
+
+    def key(name, k, b):
+        return "%s%d_%d" % (name, k, b)
+
+    def both(name, k):
+        return [key(name, k, 0), key(name, k, 1)]
+
+    def probe(k, b):
+        i = 2 * k + b
+        tt(T.pk[:, i, 0:32], T.st[:, sti(k + 1, b) + 2, :], T.sg[:, i, :], ALU.mult,
+           [key("sm", k + 1, b), key("sg", k, b)], [key("sh", k, b)])
+        tt(T.w16[:, 2 + i, 0:32], T.st[:, sti(k, b), :], T.pk[:, i, 0:32], ALU.add,
+           [key("mb", k, b), key("sh", k, b)], [key("w", k + 1, b)])
+
+    def half(k, b):
+        ts(T.st[:, sti(k + 1, b) + 2, :], T.st[:, sti(k, b) + 1, :], 1, 0xFFFE, ALU.arith_shift_right, ALU.bitwise_and,
+           [key("mb", k, b)], [key("sm", k + 1, b)])
+
+    def later(k, b):
+        i = 2 * k + b
+        if k < RO:
+            tt(T.pk[:, i, 32:64], T.dx[:, i, :], T.st[:, sti(k + 1, b) + 2, :], ALU.subtract,
+               [key("dx", k, b), key("sm", k + 1, b)], [key("db", k, b)])
+        else:
+            ts(T.mu[:, b, :], T.st[:, sti(k, b), :], C0, None, ALU.add, None, [key("mb", k, b)], [key("mu", 0, b)])
+
+    def rows(k, j):
+        return T.st[:, sti(k, 0) + j:sti(k, 1) + j + 1:3, :]
+
+    for b in range(2):
+        cp(T.nn[:, b, :], T.n32[:, :, 16 * b:16 * b + 16], ["n32"], [key("nn", 0, b)])
+    NN = both("nn", 0)
+    ts(T.tmp[:, 0:2, :], T.nn[:], 1, None, ALU.arith_shift_right, None, NN, ["m0"])
+    ts(T.w16[:, 0:2, 0:32], T.nn[:], C0, None, ALU.subtract, None, NN, both("w", 0))
+    ts(T.w16[:, 2:4, 0:32], T.tmp[:, 0:2, :], C0, None, ALU.subtract, None, ["m0"], both("w", 1))
+    for j in range(4):
+        mm(T.po[0:33, 128 * j:128 * j + 128], T.w16[:, j, 0:33], T.idh[:], True, True,
+           [key("w", j // 2, j % 2), "idh", "w16c"], ["po"])
+
+    def selo(i):
+        ts(T.selo[:, i, :], T.kk[:], float(128 * (i % 2) - 16 * (i // 2)), None, ALU.is_equal, None, ["kk"], ["selo%d" % i])
+    for i in range(4):
+        selo(i)
+    cp(T.t2[0:33, 0:4, :], T.po[0:33, :], ["po"], both("t2", 0) + both("t2", 1))
+    for i in range(4, 16):
+        selo(i)
+
+    def spread(buf, bank, j, b, c, h):
+        for i in range(4):
+            ch = 8 * c + 4 * h + i
+            mm(buf[:, 128 * i:128 * i + 128], T.selt[0:33, ch, :], T.t2[0:33, 2 * j + b, :], True, True,
+               ["selt%d" % ch, key("t2", j, b)], [bank])
+
+    def to_lists(buf, bank, c0, j, b, stop):
+        for a in range(8):
+            for s in range(2):
+                mm(buf[:, c0 + a:c0 + 128:8], T.selo[:, 2 * a + s, :], T.w16[:, 2 * j + b, 16 * s:16 * s + 16], False,
+                   stop and a == 7 and s == 1, ["selo%d" % (2 * a + s), key("w", j, b)], [bank])
+
+    free = ((T.pa[:, 0:512], "pa0"), (T.pa[:, 512:1024], "pa1"), (T.pb0[:, 512:1024], "pb01"),
+            (T.pb1[:, 0:512], "pb10"), (T.pb1[:, 512:1024], "pb11"))
+
+    def lengths(hh):
+        buf, bank = free[hh % 5]
+        spread(buf, bank, 0, hh // 4, (hh // 2) % 2, hh % 2)
+        act(T.nb[:, 512 * hh:512 * hh + 512], buf, ACT.Copy, [bank], ["nb%d" % hh])
+
+    first = ((T.pg, "pg"), (T.pb0, "pb00"))
+    for hh in range(5):
+        lengths(hh)
+    for j in range(2):
+        buf, bank = first[j]
+        mm(buf[:, 0:256], T.idh[:], T.zero[:], True, False, ["idh", "zero"], [bank])
+        for b in range(2):
+            to_lists(buf, bank, 128 * b, j, b, False)
+    for hh in range(5, 8):
+        lengths(hh)
+
+    ts(T.tmp[:, 2:4, :], T.nn[:], 1, None, ALU.bitwise_and, None, NN, ["odd"])
+    ts(rows(1, 2), T.nn[:], 0xFFFE, None, ALU.bitwise_and, None, NN, both("sm", 1))
+    ts(rows(1, 0), T.tmp[:, 0:2, :], C0, None, ALU.subtract, None, ["m0"], ["m1"])
+    tt(rows(1, 1), T.nn[:], T.tmp[:, 2:4, :], ALU.add, NN + ["odd", "m1"], both("mb", 1))
+    ts(T.dx[:, 2:4, :], T.tmp[:, 2:4, :], 2.0, None, ALU.mult, None, ["odd"], both("dx", 1))
+    ts(T.sg[:, 2:4, :], T.tmp[:, 2:4, :], 0.5, None, ALU.subtract, None, ["odd"], both("sg", 1))
+    ts(T.pbit[:], T.pcol[:], 4, 1, ALU.arith_shift_right, ALU.bitwise_and, ["pcol"], ["pbit"])
+    for b in range(2):
+        half(1, b)
+    cp(T.pflt[:], T.pbit[:], ["pbit"], ["pflt"])
+    for b in range(2):
+        probe(1, b)
+        later(1, b)
+    tt(T.ind[:], T.srow[:], T.pflt[:], ALU.is_equal, ["srow", "pflt"], ["ind"])
+
+    for i, x in enumerate(peers):
+        for s in range(2):
+            c = (2 * (r ^ x) + s) * 32
+            dma("s", T.lo32[:, c:c + 32], T.lld[i, 64 * s:64 * s + 64, :], [], ["lo32"], "lold", 128, [("larr", 8)])
+    for s, i in ((0, 0), (0, 1), (0, 2), (1, 1), (1, 0), (1, 2)):
+        row = 32 * (r ^ peers[i]) + 16 * s
+        dma("s", T.win[row:row + 16, :], T.wld[3 * s + i], [], ["win"], "winld", 112,
+            [("warr%d" % (3 * s + i), deal[s][i][1])])
+
+    ts(T.loc[:], T.lo32[:], C0, None, ALU.subtract, None, ["lo32"], ["loc"])
+    for q in range(N):
+        for a in range(8):
+            for s in range(2):
+                c = (2 * q + s) * 32
+                mm(T.po[32 * q:32 * q + 32, a:256:8], T.selo[:, 2 * a + s, 32 * q:32 * q + 32], T.loc[:, c:c + 32],
+                   s == 0, s == 1, ["selo%d" % (2 * a + s), "loc"], ["po"])
+    cp(T.log[:], T.po[:, 0:256], ["po"], ["log"])
+    ts(T.off[:, 0:256], T.po[:, 0:256], C0, None, ALU.add, None, ["po"], both("off", 0))
+    for j in range(2):
+        buf, bank = first[j]
+        mm(buf[:, 0:256], T.idh[:], T.log[:], False, True, ["idh", "log"], [bank])
+        ts(T.off[:, 256 * (j + 1):256 * (j + 2)], buf[:, 0:256], 2 * C0, None, ALU.add, None, [bank], both("off", j + 1))
+
+    PB = (T.pb0, T.pb1)
+
+    def picked(slot, hh, k):
+        c = 256 * slot + 32 * hh
+        return T.win[:].indirect(T.off[:, c:c + 32 * k])
+
+    def gather(n, h):
+        hh = 2 * (n % 4) + h
+        act(T.xg[:, 512 * hh:512 * hh + 512], picked(n // 4 + 2, hh, 1), ACT.Copy,
+            ["win", key("off", n // 4 + 2, hh // 4)], ["x%d" % hh])
+
+    def gather0(n):
+        for h in range(2):
+            hh = 2 * n + h
+            act(T.s0[:, 512 * hh:512 * hh + 512], picked(0, hh, 1), ACT.Copy, ["win", key("off", 0, hh // 4)], ["s0%d" % hh])
+
+    def rise(n):
+        for hh, k in (((0, 1), (1, 1)) if n == 0 else ((2 * n, 2),)):
+            sl = slice(512 * hh, 512 * (hh + k))
+            tt(T.rise[:, sl], picked(1, hh, k), T.s0[:, sl], ALU.subtract,
+               ["win", key("off", 1, hh // 4)] + ["s0%d" % (hh + i) for i in range(k)], ["r%d" % (hh + i) for i in range(k)])
+
+    def places(n):
+        for h in range(2):
+            spread(PB[n % 2][:, 512 * h:512 * h + 512], "pb%d%d" % (n % 2, h), n // 4 + 1, (n % 4) // 2, n % 2, h)
+
+    def moved(n, h):
+        return n % 2 == 0 and h < OFF
+
+    def ycol(n):
+        return 2048 if n % 2 else 512 * (n % 4)
+
+    def lifted(n, h):
+        hh = 2 * (n % 4) + h
+        sl = slice(512 * hh, 512 * hh + 512)
+        m0, m1 = (T.idb, T.nid) if moved(n, h) else (T.nid, T.idb)
+        mm(T.pa[:, 512 * h:512 * h + 512], m0[:], T.s0[:, sl], True, False, ["nid", "idb", "s0%d" % hh], ["pa%d" % h])
+        mm(T.pa[:, 512 * h:512 * h + 512], m1[:], T.xg[:, sl], False, True, ["x%d" % hh], ["pa%d" % h])
+
+    adds = {}
+
+    def add(u):
+        sem = "acc%d" % (u // 512)
+        adds[sem] = adds.get(sem, 0) + 16
+        op("g", lambda: g.dma_start(T.yy[:, u:u + 512], T.uu[:, u:u + 512], accum_op=ALU.add), ["u%d" % u, "y%d" % u],
+           ["y%d" % u], sem, adds[sem])
+
+    def v1(n):
+        c = n % 4
+        y = ycol(n)
+        tt(T.yy[:, y:y + 1024], T.pa[:], T.nb[:, 1024 * c:1024 * c + 1024], ALU.mult,
+           ["pa0", "pa1", "nb%d" % (2 * c), "nb%d" % (2 * c + 1)], ["y%d" % y, "y%d" % (y + 512)])
+        for h in range(2):
+            if moved(n, h):
+                add(y + 512 * h)
+
+    def v2(n):
+        c = n % 4
+        y = ycol(n)
+        k = OFF if n % 2 == 0 else 0
+        for h0, h1 in ((0, k), (k, 2)):
+            if h0 < h1:
+                banks = ["pb%d%d" % (n % 2, h) for h in range(h0, h1)]
+                src = PB[n % 2][:, 512 * h0:512 * h1]
+                away = moved(n, h0)
+                tt(T.uu[:, y + 512 * h0:y + 512 * h1] if away else src, src,
+                   T.rise[:, 1024 * c + 512 * h0:1024 * c + 512 * h1], ALU.mult,
+                   banks + ["r%d" % (2 * c + h) for h in range(h0, h1)],
+                   ["u%d" % (y + 512 * h) for h in range(h0, h1)] if away else banks)
+
+    def v3(n, split):
+        p = n % 2
+        y = ycol(n)
+        k = OFF if p == 0 else 0
+        for h0, h1 in (((0, 1), (1, 2)) if split else ((k, 2),)):
+            if h0 < h1:
+                tt(T.dd[:, 1024 * p + 512 * h0:1024 * p + 512 * h1], PB[p][:, 512 * h0:512 * h1],
+                   T.yy[:, y + 512 * h0:y + 512 * h1], ALU.subtract,
+                   ["y%d" % (y + 512 * h) for h in range(h0, h1)] + ["pb%d%d" % (p, h) for h in range(h0, h1)],
+                   ["d%d%d" % (p, h) for h in range(h0, h1)])
+
+    def sizes(n, h):
+        if moved(n, h):
+            return T.yy, ycol(n) + 512 * h, "y%d" % (ycol(n) + 512 * h)
+        return T.dd, 1024 * (n % 2) + 512 * h, "d%d%d" % (n % 2, h)
+
+    def size(n, h):
+        buf, c, kd = sizes(n, h)
+        act(buf[:, c:c + 512], buf[:, c:c + 512], ACT.Abs, [kd], [kd])
+
+    def total(n, h):
+        b = (n % 4) // 2
+        buf, c, kd = sizes(n, h)
+        for i in range(4):
+            ch = 8 * (n % 2) + 4 * h + i
+            mm(T.pg[:, 64 * b + ch:64 * b + 64:16], buf[:, c + 128 * i:c + 128 * i + 128], T.ind[:], True, True,
+               [kd, "ind"], ["pg"])
+
+    def decide(k, b):
+        i = 2 * k + b
+        gw = T.pg[:, 64 * b:64 * b + 64]
+        if k == 0:
+            cp(T.gm[:, 2 + b, :], gw, ["pg"], [key("gm", 1, b)])
+            return
+        if k == RO:
+            gw = T.pg[:, 64 * b:64 * b + 32]
+            tt(T.up[:, i, 0:32], gw, T.gm[:, i, 0:32], ALU.is_gt, ["pg", key("gm", k, b)], [key("up", k, b)])
+            tt(T.res[:, b, 2:4, :], gw, T.gm[:, i, 0:32], ALU.max, ["pg", key("gm", k, b)], [key("rg", 0, b)])
+            tt(T.dl[:, i, 0:32], T.up[:, i, 0:32], T.pk[:, i, 0:32], ALU.mult, [key("up", k, b), key("sh", k, b)], [key("dl", k, b)])
+            tt(T.res[:, b, 0:2, :], T.mu[:, b, :], T.dl[:, i, 0:32], ALU.add, [key("mu", 0, b), key("dl", k, b)], [key("rm", 0, b)])
+            send([(x, deal[b][j][0], deal[b][j][1], T.res[:, b, :, :], T.rld[:, 2 * j + b, :, :], "rarr%d" % j)
+                  for j, x in enumerate(peers)], [key("rg", 0, b), key("rm", 0, b)])
+            return
+        i1 = i + 2
+        tt(T.up[:, i, :], gw, T.gm[:, i, :], ALU.is_gt, ["pg", key("gm", k, b)], [key("up", k, b)])
+        tt(T.gm[:, i1, :], gw, T.gm[:, i, :], ALU.max, ["pg", key("gm", k, b)], [key("gm", k + 1, b)])
+        tt(T.dl[:, i, :], T.up[:, i, :], T.pk[:, i, :], ALU.mult,
+           [key("up", k, b), key("sh", k, b), key("db", k, b)], [key("dl", k, b)])
+        tt(T.st[:, sti(k + 1, b):sti(k + 1, b) + 2, :], T.st[:, sti(k, b):sti(k, b) + 3:2, :], T.dl[:, i, :], ALU.add,
+           [key("mb", k, b), key("sm", k, b), key("dl", k, b)], [key("mb", k + 1, b)])
+        tt(T.tau[:, i, :], T.dl[:, i, 0:32], T.sg[:, i, :], ALU.subtract, [key("dl", k, b), key("sg", k, b)], [key("tau", k, b)])
+        tt(T.dx[:, i1, :], T.st[:, sti(k + 1, b) + 1, :], T.st[:, sti(k + 1, b) + 2, :], ALU.subtract,
+           [key("mb", k + 1, b), key("sm", k + 1, b)], [key("dx", k + 1, b)])
+        half(k + 1, b)
+        tt(T.qq[:, i, :], T.dx[:, i1, :], T.tau[:, i, :], ALU.mult, [key("dx", k + 1, b), key("tau", k, b)], [key("qq", k, b)])
+        ts(T.sg[:, i1, :], T.qq[:, i, :], 0.0, 0.5, ALU.is_gt, ALU.subtract, [key("qq", k, b)], [key("sg", k + 1, b)])
+        probe(k + 1, b)
+
+    def lists(k, b):
+        if k < RO:
+            j = k + 2
+            mm(T.po[:, 0:128], T.idh[:], T.log[:, 128 * b:128 * b + 128], True, False, ["idh", "log"], ["po"])
+            to_lists(T.po, "po", 0, j, b, True)
+            mm(T.po[0:33, 128:256], T.w16[:, 2 * j + b, 0:33], T.idh[:], True, True, [key("w", j, b), "idh"], ["po"])
+
+    def publish(k, b, part):
+        if k < RO:
+            j = k + 2
+            c = 256 * (j + 1) + 128 * b
+            if part == 0:
+                ts(T.off[:, c:c + 128], T.po[:, 0:128], 2 * C0, None, ALU.add, None, ["po"], [key("off", j + 1, b)])
+            else:
+                cp(T.t2[0:33, 2 * j + b, :], T.po[0:33, 128:256], ["po"], [key("t2", j, b)])
+
+    def at(i, name, step, *args):
+        place[0] = (i, name)
+        step(*args)
+
+    def ahead(i, n):
+        if n < 4:
+            at(i, "gx0", gather0, n)
+        at(i, "gx0", gather, n, 0)
+        at(i, "gx1", gather, n, 1)
+        at(i, "px", places, n)
+        at(i, "lx0", lifted, n, 0)
+        at(i, "lx1", lifted, n, 1)
+        if n < 4:
+            at(i, "v2x", rise, n)
+        at(i, "v2x", v2, n)
+
+    slots = 2 * (RO + 1)
+    ahead(-1, 0)
+    for i in range(slots):
+        n0, n1 = 2 * i, 2 * i + 1
+        k, b = (i - 1) // 2, (i - 1) % 2
+        more = i + 1 < slots
+        at(i, "p1", places, n1)
+        at(i, "v1a", v1, n0)
+        if n1 < 4:
+            at(i, "g10", gather0, n1)
+        at(i, "g10", gather, n1, 0)
+        at(i, "g11", gather, n1, 1)
+        if n1 < 4:
+            at(i, "v2b", rise, n1)
+        at(i, "v2b", v2, n1)
+        at(i, "l10", lifted, n1, 0)
+        at(i, "l11", lifted, n1, 1)
+        if i > 0:
+            at(i, "dec", decide, k, b)
+            at(i, "lis", lists, k, b)
+            at(i, "pu0", publish, k, b, 0)
+            at(i, "pu1", publish, k, b, 1)
+            if 1 <= k < RO:
+                at(i, "lat", later, k + 1, b)
+        at(i, "v3a", v3, n0, False)
+        at(i, "v1b", v1, n1)
+        if more:
+            ahead(i, n1 + 1)
+        at(i, "v3b", v3, n1, SPLIT or not more)
+        for n, name in ((n0, "a"), (n1, "b")):
+            for h in range(2):
+                at(i, "s%s%d" % (name, h), size, n, h)
+                at(i, "t%s%d" % (name, h), total, n, h)
+    at(slots + 1, "dec", decide, RO, 1)
+
+    RES = both("rg", 0) + both("rm", 0)
+    outs = (T.ym, T.yg)
+    for t in range(2):
+        for s in range(2):
+            row = 32 * r + 16 * s
+            dma("s" if s == 0 else "a", outs[t][row:row + 16, :], T.res[:, :, 2 * t + s, :], RES, [], "outs", 256)
+    for i, x in enumerate(peers):
+        for t in range(2):
+            for s in range(2):
+                row = 32 * (r ^ x) + 16 * s
+                dma("s" if s == 0 else "a", outs[t][row:row + 16, :], T.rld[:, 2 * i:2 * i + 2, 2 * t + s, :], RES, [],
+                    "outs", 256, [("rarr%d" % i, deal[0][i][1] + deal[1][i][1])])
+
+    for i in arrange():
+        emit(plan[i])
+    wait("g", "sent", sent[0])
+    for q in cnt:
+        wait("g", "c" + q, cnt[q])
+    for s in sorted(totals):
+        wait("g", s, totals[s])

@@ -6,72 +6,188 @@ ACT = ActivationFunctionType
 N = 4
 RO = 6
 C0 = 2048.0
-OFF = 0
-SPLIT = False
-PLACE = {'p1': -0.677, 'sb0': -2.356, 'tb0': -4.084, 'sb1': -0.146, 'tb1': -2.441, 'v1a': 0.232, 'g10': 0.361,
-         'g11': 0.518, 'v2b': 0.234, 'l10': -2.037, 'l11': 0.239, 'dec': 0.265, 'lis': 0.455, 'v3a': 0.34,
-         'pu0': -3.317, 'pu1': -2.806, 'sa0': 0.614, 'gx0': 0.67, 'gx1': 0.859, 'v1b': 0.976, 'px': 0.546,
-         'ta0': -2.262, 'lx0': -0.518, 'lx1': 0.081, 'lat': 1.978, 'v2x': 1.195, 'sa1': 0.978, 'ta1': 1.029,
-         'v3b': 0.995}
+KK = 4096.0
+AWAY = ((0, 4), (4, 6))
+ADDED = {e: (AWAY, (), AWAY, ()) for e in range(1, RO)}
+RUNS = (((0, 8),), ((0, 4), (4, 8)))
+LAST = ((0, 4), (4, 8))
+FIRST_ON_V = (1, 3)
+CYC, PE, GATHER, SEM, VFIX, AFIX = 0.83, 0.42, 1.56, 70.0, 40.0, 65.0
+LOOK = {"v": 150.0, "a": 150.0, "p": 150.0, "g": 0.0, "s": 0.0}
+LANDS = {"lo": 13000.0, "walk": 17000.0, "res": 3500.0, "add": 2000.0, "add+": 400.0}
+SWEEPS = 2
+FIXED = 99
+RANK = {"g00": 0.0, "g01": 0.0, "t00": 0.0, "t01": 0.0, "s00": 0.0, "s01": 0.0, "l00": 0.0, "l01": 0.0,
+        "u0": 0.0, "y00": 0.0, "y01": 0.0, "y02": 0.0, "d00": 0.0, "a00": 0.55, "a01": 0.55,
+        "g10": 0.5, "g11": 0.5, "t10": 0.5, "t11": 0.5, "s10": 0.5, "s11": 0.5, "l10": 0.5, "l11": 0.5,
+        "u1": 0.5, "y10": 0.5, "d10": 0.5, "d11": 0.5, "a10": 0.6, "a11": 0.6, "h0": 0.7, "h1": 0.7,
+        "m00": 0.55, "m01": 0.55, "m10": 0.6, "m11": 0.6, "mh0": 0.7, "mh1": 0.7,
+        "up": 0.8, "dl": 0.8, "st": 0.8, "tau": 0.8, "dx": 0.8, "hf": 0.8, "qq": 0.8, "gm": 0.8, "sg": 0.8, "sh": 0.8,
+        "w": 0.8, "trn": 0.8, "lis": 0.8, "off": 0.8, "t2": 0.8, "end": -0.74, "fst": 0.0, "fsum": 0.43}
 
 SCRATCH = {
     "wst": ("dram", [6, 128, 512], "bfloat16"),
     "wld": ("dram", [6, 128, 512], "bfloat16"),
-    "lst": ("dram", [4, 128, 64], "int32"),
-    "lld": ("dram", [3, 128, 64], "int32"),
-    "res": ("sbuf", [128, 2, 4, 16], "float32"),
-    "rld": ("sbuf", [128, 6, 4, 16], "float32"),
+    "los": ("sbuf", [128, 8, 32], "float16"),
+    "loc": ("sbuf", [128, 8, 32], "float16"),
+    "res": ("sbuf", [128, 2, 64], "float32"),
+    "rs": ("sbuf", [128, 2, 64], "float32"),
+    "rld": ("sbuf", [128, 6, 64], "float32"),
     "win": ("sbuf", [128, 4096], "bfloat16"),
     "xg": ("sbuf", [128, 4096], "bfloat16"),
+    "xz": ("sbuf", [128, 4096], "bfloat16"),
     "s0": ("sbuf", [128, 4096], "bfloat16"),
     "rise": ("sbuf", [128, 4096], "bfloat16"),
     "nb": ("sbuf", [128, 4096], "float32"),
-    "yy": ("sbuf", [128, 3072], "float32"),
-    "uu": ("sbuf", [128, 2048], "float32"),
-    "dd": ("sbuf", [128, 2048], "float32"),
+    "yy": ("sbuf", [128, 4096], "float32"),
+    "uu": ("sbuf", [128, 4096], "float32"),
+    "dd": ("sbuf", [128, 3072], "float32"),
     "jj": ("sbuf", [128, 128], "bfloat16"),
     "kk": ("sbuf", [128, 128], "bfloat16"),
     "kt": ("sbuf", [128, 128], "bfloat16"),
     "pcol": ("sbuf", [128, 4], "int32"),
     "pbit": ("sbuf", [128, 4], "int32"),
-    "pflt": ("sbuf", [128, 4], "float32"),
     "srow": ("sbuf", [128, 4], "float32"),
     "ind": ("sbuf", [128, 4], "float32"),
-    "idb": ("sbuf", [128, 128], "bfloat16"),
-    "nid": ("sbuf", [128, 128], "bfloat16"),
+    "ind0": ("sbuf", [128, 4], "float32"),
+    "dia": ("sbuf", [128, 5, 128], "bfloat16"),
     "idh": ("sbuf", [128, 128], "float16"),
+    "idf": ("sbuf", [128, 128], "float32"),
     "selo": ("sbuf", [128, 16, 128], "float16"),
     "selt": ("sbuf", [128, 16, 128], "float16"),
-    "zero": ("sbuf", [128, 256], "float16"),
-    "n32": ("sbuf", [128, 2, 32], "int32"),
+    "n32": ("sbuf", [128, 256], "int32"),
     "lo32": ("sbuf", [128, 256], "int32"),
-    "loc": ("sbuf", [128, 256], "float16"),
+    "loh": ("sbuf", [128, 256], "float16"),
     "log": ("sbuf", [128, 256], "float16"),
     "off": ("sbuf", [128, 9 * 256], "uint16"),
     "t2": ("sbuf", [128, 16, 128], "float16"),
     "nn": ("sbuf", [128, 2, 32], "int32"),
     "tmp": ("sbuf", [128, 4, 32], "int32"),
     "st": ("sbuf", [128, 48, 32], "int32"),
-    "pk": ("sbuf", [128, 16, 64], "float32"),
+    "wk": ("sbuf", [128, 64, 32], "float16"),
     "sg": ("sbuf", [128, 16, 32], "float32"),
-    "up": ("sbuf", [128, 16, 64], "float32"),
-    "dl": ("sbuf", [128, 16, 64], "float32"),
     "gm": ("sbuf", [128, 16, 64], "float32"),
     "tau": ("sbuf", [128, 16, 32], "float32"),
-    "dx": ("sbuf", [128, 16, 32], "float32"),
     "qq": ("sbuf", [128, 16, 32], "float32"),
     "mu": ("sbuf", [128, 2, 32], "float32"),
-    "w16": ("sbuf", [128, 16, 40], "float16"),
+    "ee": ("sbuf", [128, 2, 64], "float32"),
+    "cf": ("sbuf", [128, 2, 64], "float32"),
+    "ci": ("sbuf", [128, 2, 64], "int32"),
+    "g0": ("sbuf", [128, 6, 64], "float32"),
     "pa": ("psum", [128, 1024], "float32"),
     "pb0": ("psum", [128, 1024], "float32"),
     "pb1": ("psum", [128, 1024], "float32"),
-    "pg": ("psum", [128, 512], "float32"),
-    "po": ("psum", [128, 512], "float32"),
+    "pg0": ("psum", [128, 512], "float32"),
+    "pg1": ("psum", [128, 512], "float32"),
 }
-SEMAPHORES = (["cv", "ca", "cp", "cg", "sent", "lstg", "wstg0", "wstg1", "larr", "nld", "lold", "winld", "outs"]
-              + ["warr%d" % k for k in range(6)] + ["rarr%d" % k for k in range(3)] + ["acc%d" % k for k in range(4)])
+NACC = 6
+SEMAPHORES = (["cv", "ca", "cp", "cg", "sent", "wstg0", "wstg1", "larr", "nld", "lold", "winld", "outs"]
+              + ["warr%d" % k for k in range(6)] + ["rarr%d" % k for k in range(6)] + ["acc%d" % k for k in range(NACC)])
 
-PSUM_KEYS = ("pa0", "pa1", "pb00", "pb01", "pb10", "pb11", "pg", "po")
+PSUM_KEYS = ("pa0", "pa1", "pb00", "pb01", "pb10", "pb11", "pg0", "pg1")
+ORDER = []
+
+
+def width(ap):
+    n = 1
+    for d in ap.shape[1:]:
+        n *= d
+    return n
+
+
+def arrange(plan):
+    n = len(plan)
+    before = [set() for _ in range(n)]
+    wr, rd, last, gate = {}, {}, {}, {}
+    for i, o in enumerate(plan):
+        for k in o["reads"]:
+            before[i].update(wr.get(k, ()))
+            if k in PSUM_KEYS:
+                before[i].update(j for j in rd.get(k, ()) if plan[j]["q"] != o["q"])
+        if o["join"]:
+            k = o["writes"][0]
+            if rd.get(k) or not plan[wr[k][-1]]["join"]:
+                gate[k], wr[k], rd[k] = wr[k] + rd[k], [], []
+            before[i].update(gate[k])
+            wr[k].append(i)
+            for k in o["reads"]:
+                rd.setdefault(k, []).append(i)
+            continue
+        if not o["fresh"]:
+            for k in o["writes"]:
+                before[i].update(wr.get(k, ()))
+                before[i].update(rd.get(k, ()))
+        if o["q"] in "gs" or o["sem"] is not None:
+            if o["q"] in last:
+                before[i].add(~last[o["q"]])
+            last[o["q"]] = i
+        for k in o["reads"]:
+            rd.setdefault(k, []).append(i)
+        for k in o["writes"]:
+            if o["fresh"]:
+                wr.setdefault(k, []).append(i)
+            else:
+                wr[k] = [i]
+                rd[k] = []
+        before[i].discard(i)
+    after = [[] for _ in range(n)]
+    ahead = [[] for _ in range(n)]
+    for i in range(n):
+        for j in before[i]:
+            gap = 0.0
+            if j >= 0 and not (plan[i]["q"] == "p" == plan[j]["q"]):
+                gap = plan[j]["late"] + SEM
+            j = j if j >= 0 else ~j
+            after[j].append((i, gap))
+            ahead[i].append((j, gap))
+
+    left = [len(x) for x in ahead]
+    ready, last, links = [i for i in range(n) if left[i] == 0], {}, []
+    while ready:
+        i = min(ready, key=lambda i: (plan[i]["rank"], i))
+        ready.remove(i)
+        if plan[i]["fixed"]:
+            if plan[i]["q"] in last:
+                links.append((last[plan[i]["q"]], i))
+            last[plan[i]["q"]] = i
+        for j, gap in after[i]:
+            left[j] -= 1
+            if left[j] == 0:
+                ready.append(j)
+    for j, i in links:
+        after[j].append((i, 0.0))
+        ahead[i].append((j, 0.0))
+
+    def sweep(nxt, prev, can, weight):
+        left = [len(x) for x in prev]
+        ready = {q: [] for q in LOOK}
+        for i in range(n):
+            if left[i] == 0:
+                ready[plan[i]["q"]].append(i)
+        free = {q: 0.0 for q in LOOK}
+        out, end = [], [0.0] * n
+        while len(out) < n:
+            t, q = min((max(free[q], min(can[i] for i in ready[q])), q) for q in LOOK if ready[q])
+            i = max((i for i in ready[q] if can[i] <= t + LOOK[q]), key=lambda i: (weight[i], -i))
+            ready[q].remove(i)
+            out.append(i)
+            end[i] = free[q] = max(t, can[i]) + plan[i]["busy"]
+            for j, gap in nxt[i]:
+                can[j] = max(can[j], end[i] + gap)
+                left[j] -= 1
+                if left[j] == 0:
+                    ready[plan[j]["q"]].append(j)
+        return out, end
+
+    weight = [-o["rank"] for o in plan]
+    best = None
+    for k in range(SWEEPS):
+        out, end = sweep(after, ahead, [o["at"] for o in plan], weight)
+        if best is None or max(end) < best[0]:
+            best = (max(end), out)
+        if k + 1 < SWEEPS:
+            weight = sweep(ahead, after, [o["late"] for o in plan], end)[1]
+    return best[1]
 
 
 def rank_program(g, core, T, topo):
@@ -80,56 +196,15 @@ def rank_program(g, core, T, topo):
         return
     Q = {"v": g.vector, "a": g.scalar, "p": g.tensor, "g": g, "s": g.sync}
     plan = []
-    place = [(-9, "dec")]
+    here = [-9.0, None, None]
 
-    def op(q, call, reads, writes, sem=None, total=0, fresh=False, pre=()):
+    def op(q, call, reads, writes, busy, sem=None, total=0, fresh=False, pre=(), late=0.0, at=0.0, join=False):
         plan.append(dict(q=q, call=call, reads=reads, writes=writes, sem=sem, total=total, fresh=fresh, pre=pre,
-                         at=place[0]))
+                         busy=busy, late=late, at=at, rank=here[0], join=join, slot=here[1], tag=here[2],
+                         fixed=here[1] is not None and here[0] >= FIXED))
 
-    def arrange():
-        n = len(plan)
-        before = [set() for _ in range(n)]
-        wr, rd, last = {}, {}, {}
-        for i, o in enumerate(plan):
-            for k in o["reads"]:
-                before[i].update(wr.get(k, ()))
-                if k in PSUM_KEYS:
-                    before[i].update(j for j in rd.get(k, ()) if plan[j]["q"] != o["q"])
-            if not o["fresh"]:
-                for k in o["writes"]:
-                    before[i].update(wr.get(k, ()))
-                    before[i].update(rd.get(k, ()))
-            if o["q"] in "gs" or o["sem"] is not None:
-                if o["q"] in last:
-                    before[i].add(~last[o["q"]])
-                last[o["q"]] = i
-            for k in o["reads"]:
-                rd.setdefault(k, []).append(i)
-            for k in o["writes"]:
-                if o["fresh"]:
-                    wr.setdefault(k, []).append(i)
-                else:
-                    wr[k] = [i]
-                    rd[k] = []
-            before[i].discard(i)
-        after = [[] for _ in range(n)]
-        left = [0] * n
-        for i in range(n):
-            for j in set(j if j >= 0 else ~j for j in before[i]):
-                after[j].append(i)
-                left[i] += 1
-        rank = [(o["at"][0] + PLACE[o["at"][1]], i) for i, o in enumerate(plan)]
-        ready = [rank[i] for i in range(n) if left[i] == 0]
-        out = []
-        while ready:
-            ready.sort()
-            i = ready.pop(0)[1]
-            out.append(i)
-            for j in after[i]:
-                left[j] -= 1
-                if left[j] == 0:
-                    ready.append(rank[j])
-        return out
+    def step(e, b, name, more=0.0):
+        here[:] = [2 * e + b + RANK[name] + more, 2 * e + b, name]
 
     cnt = {"v": 0, "a": 0, "p": 0, "g": 0}
     seen = {q: {} for q in Q}
@@ -179,30 +254,37 @@ def rank_program(g, core, T, topo):
             writer[k] = mark
             readers[k] = {}
 
-    def dma(q, out, in_, reads, writes, sem, total, pre=()):
-        op(q, lambda: Q[q].dma_start(out, in_), reads, writes, sem, total, True, pre)
+    def dma(q, out, in_, reads, writes, sem, total, pre=(), at=0.0):
+        op(q, lambda: Q[q].dma_start(out, in_), reads, writes, 60.0, sem, total, True, pre, 2000.0, at)
+
+    def vcost(n):
+        return VFIX + max(64.0, n) * CYC
 
     def tt(out, a, b, alu, reads, writes):
-        op("v", lambda: g.vector.tensor_tensor(out, a, b, alu), reads, writes)
+        n = width(out) * (1.0 if any(k in PSUM_KEYS for k in reads) else 2.0)
+        op("v", lambda: g.vector.tensor_tensor(out, a, b, alu), reads, writes, vcost(n))
 
     def ts(out, a, s1, s2, o0, o1, reads, writes):
+        n = width(out) / (2 if reads[0] in ("jj", "kk", "kt") else 1)
         if o1 is None:
-            op("v", lambda: g.vector.tensor_scalar(out, a, s1, None, o0), reads, writes)
+            op("v", lambda: g.vector.tensor_scalar(out, a, s1, None, o0), reads, writes, vcost(n))
         else:
-            op("v", lambda: g.vector.tensor_scalar(out, a, s1, s2, o0, o1), reads, writes)
+            op("v", lambda: g.vector.tensor_scalar(out, a, s1, s2, o0, o1), reads, writes, vcost(n))
 
     def cp(out, a, reads, writes):
-        op("v", lambda: g.vector.tensor_copy(out, a), reads, writes)
+        op("v", lambda: g.vector.tensor_copy(out, a), reads, writes, vcost(width(out)))
 
-    def mm(out, lhsT, rhs, start, stop, reads, writes):
-        op("p", lambda: g.tensor.matmul(out, lhsT, rhs, start, stop), reads, writes)
+    def mm(out, lhsT, rhs, start, stop, reads, writes, wide=False, pre=(), at=0.0, join=False):
+        c = 10.0 + max(min(64, width(lhsT)), width(rhs)) * (4 if wide else 1) * PE
+        op("p", lambda: g.tensor.matmul(out, lhsT, rhs, start, stop), reads, writes, c, pre=pre, at=at, join=join)
 
-    def act(out, a, func, reads, writes):
-        op("a", lambda: g.scalar.activation(out, a, func), reads, writes)
+    def act(out, a, func, reads, writes, gathered=False):
+        op("a", lambda: g.scalar.activation(out, a, func), reads, writes,
+           AFIX + width(out) * (GATHER if gathered else 1.0) * CYC)
 
     sent = [0]
 
-    def send(parts, reads):
+    def send(parts, reads, writes=(), late=0.0):
         trs = []
         for x, e0, ne, src, dst, sem in parts:
             peer = T.cores[r ^ x]
@@ -213,47 +295,13 @@ def rank_program(g, core, T, topo):
             trs.append(RemoteDMATransfer(dst_ids=[DstId(rid=rid, pnc=pid)], dma_engine_mask=mask,
                                          remote_sem=T.sem[sem], src=src, dst=dst))
             sent[0] += ne
-        op("g", lambda: g.remote_dma_fused(trs, local_sem=T.sem.sent), reads, [], "")
+        op("g", lambda: g.remote_dma_fused(trs, local_sem=T.sem.sent), reads, list(writes), 700.0, "", late=late)
 
     peers = (3, 1, 2)
     deal = (((0, 4), (4, 2), (6, 2)), ((0, 2), (4, 4), (2, 2)))
-
-    dma("s", T.lst[:], T.lo[:], [], ["lst"], "lstg", 16)
-    for s in range(2):
-        for i, x in enumerate(peers):
-            row = 32 * (r ^ x) + 16 * s
-            dma("s" if (s == 0) == (i != 2) else "a", T.wst[3 * s + i], T.walk[row:row + 16, :], [], ["wst%d" % s],
-                "wstg%d" % s, 48)
-    for s in range(2):
-        row = 32 * r + 16 * s
-        dma("a", T.n32[:, s, :], T.span[row:row + 16, :], [], ["n32"], "nld", 32)
-    dma("s", T.win[32 * r:32 * r + 32, :], T.walk[32 * r:32 * r + 32, :], [], ["win"], "winld", 112)
-    for s in range(2):
-        row = 32 * r + 16 * s
-        c = (2 * r + s) * 32
-        dma("a", T.lo32[:, c:c + 32], T.lo[row:row + 16, :], [], ["lo32"], "lold", 128)
-
-    op("g", lambda: g.iota(T.jj[:], [[1, 128]], 0, -1, allow_small_or_imprecise_dtypes=True), [], ["jj"])
-    op("g", lambda: g.iota(T.kt[:], [[0, 4], [16, 2], [0, 16]], 0, -1, allow_small_or_imprecise_dtypes=True), [], ["kt"])
-    op("g", lambda: g.iota(T.kk[:], [[0, 4], [128, 2], [1, 16]], 0, -1, allow_small_or_imprecise_dtypes=True), [], ["kk"])
-    op("g", lambda: g.iota(T.pcol[:], [[0, 4]], 0, 1), [], ["pcol"])
-    op("g", lambda: g.iota(T.srow[:], [[0, 2], [1, 2]], 0, 0, allow_small_or_imprecise_dtypes=True), [], ["srow"])
-
-    send([(x, deal[0][i][0], deal[0][i][1], T.lst[r ^ x], T.lld[i], "larr") for i, x in enumerate(peers)], ["lst"])
-    for s in range(2):
-        send([(x, deal[s][i][0], deal[s][i][1], T.wst[3 * s + i], T.wld[3 * s + i], "warr%d" % (3 * s + i))
-              for i, x in enumerate(peers)], ["wst%d" % s])
-
-    op("v", lambda: g.vector.memset(T.w16[:, :, 32:33], C0), [], ["w16c"])
-    op("v", lambda: g.vector.memset(T.zero[:], 0.0), [], ["zero"])
-    ts(T.idb[:], T.jj[:], 0.0, None, ALU.is_equal, None, ["jj"], ["idb"])
-    ts(T.idh[:], T.jj[:], 0.0, None, ALU.is_equal, None, ["jj"], ["idh"])
-    ts(T.nid[:], T.jj[:], 0.0, -1.0, ALU.is_equal, ALU.mult, ["jj"], ["nid"])
-    for c in range(16):
-        ts(T.selt[0:33, c, :], T.kt[0:33, :], float(-c), T.idb[0:33, 32:33], ALU.is_equal, ALU.max, ["kt", "idb"], ["selt%d" % c])
-
-    def sti(k, b):
-        return (2 * k + b) * 3
+    PG = (T.pg0, T.pg1)
+    PB = (T.pb0, T.pb1)
+    IDB, NID, BIG, NBIG, NK = (T.dia[:, j, :] for j in range(5))
 
     def key(name, k, b):
         return "%s%d_%d" % (name, k, b)
@@ -261,324 +309,362 @@ def rank_program(g, core, T, topo):
     def both(name, k):
         return [key(name, k, 0), key(name, k, 1)]
 
+    def names(x, i, j0, j1):
+        return ["%s%d%d" % (x, i, j) for j in range(j0, j1)]
+
+    dma("a", T.lo32[:], T.lo[:], [], ["lo32"], "lold", 16)
+    dma("a", T.n32[0:32, :], T.span[32 * r:32 * r + 32, :], [], ["n32"], "nld", 16)
+    for s in range(2):
+        for i, x in enumerate(peers):
+            row = 32 * (r ^ x) + 16 * s
+            dma("s", T.wst[3 * s + i], T.walk[row:row + 16, :], [], ["wst%d" % s], "wstg%d" % s, 48)
+    dma("s", T.win[32 * r:32 * r + 32, :], T.walk[32 * r:32 * r + 32, :], [], ["win"], "winld", 112)
+
+    def iota(out, pat, cm, name, **kw):
+        op("g", lambda: g.iota(out, pat, 0, cm, **kw), [], [name], 130.0 + 2 * CYC * width(out))
+    iota(T.jj[:], [[1, 128]], -1, "jj", allow_small_or_imprecise_dtypes=True)
+    iota(T.kt[:], [[0, 4], [16, 2], [0, 16]], -1, "kt", allow_small_or_imprecise_dtypes=True)
+    iota(T.kk[:], [[0, 4], [128, 2], [1, 16]], -1, "kk", allow_small_or_imprecise_dtypes=True)
+    iota(T.pcol[:], [[0, 4]], 1, "pcol")
+    iota(T.srow[:], [[0, 2], [1, 2]], 0, "srow", allow_small_or_imprecise_dtypes=True)
+
+    here[0] = -13.0
+    ts(T.idh[:], T.jj[:], 0.0, None, ALU.is_equal, None, ["jj"], ["idh"])
+    ts(T.loh[:], T.lo32[:], C0, None, ALU.subtract, None, ["lo32"], ["loh"])
+    for b in range(2):
+        mm(T.pg0[:, 128 * b:128 * b + 128], T.loh[:, 128 * b:128 * b + 128], T.idh[:], True, True, ["loh", "idh"], ["pg0"])
+    for b in range(2):
+        cp(T.los[:, :, 16 * b:16 * b + 16], T.pg0[:, 128 * b:128 * b + 128], ["pg0"], ["los%d" % b])
+
+    def walks(s):
+        send([(x, deal[s][i][0], deal[s][i][1], T.wst[3 * s + i], T.wld[3 * s + i], "warr%d" % (3 * s + i))
+              for i, x in enumerate(peers)], ["wst%d" % s])
+    walks(0)
+    send([(x, deal[0][i][0], deal[0][i][1], T.los[:, 2 * (r ^ x):2 * (r ^ x) + 2, :], T.loc[:, 2 * r:2 * r + 2, :], "larr")
+          for i, x in enumerate(peers)], ["los0", "los1"])
+    walks(1)
+    for s, i in ((0, 0), (0, 1), (0, 2), (1, 1), (1, 0), (1, 2)):
+        row = 32 * (r ^ peers[i]) + 16 * s
+        dma("s", T.win[row:row + 16, :], T.wld[3 * s + i], [], ["win"], "winld", 112,
+            [("warr%d" % (3 * s + i), deal[s][i][1])], LANDS["walk"] - 2000.0)
+
+    here[0] = -12.0
+    op("v", lambda: g.vector.memset(T.t2[32:33, :, :], C0), [], ["t2c"], vcost(1024))
+    for j, c in enumerate((1.0, -1.0, 2 * KK, -2 * KK, -KK)):
+        ts(T.dia[:, j, :], T.jj[:], 0.0, c, ALU.is_equal, ALU.mult, ["jj"], ["dia%d" % j])
+    for i in range(16):
+        ts(T.selo[:, i, :], T.kk[:], float(128 * (i % 2) - 16 * (i // 2)), None, ALU.is_equal, None, ["kk"], ["selo%d" % i])
+    here[0] = -10.0
+    for c in range(16):
+        ts(T.selt[0:33, c, :], T.kt[0:33, :], float(-c), T.dia[0:33, 0, 32:33], ALU.is_equal, ALU.max, ["kt", "dia0"],
+           ["selt%d" % c])
+    ts(T.idf[:], T.jj[:], 0.0, None, ALU.is_equal, None, ["jj"], ["idf"])
+    ts(T.pbit[:], T.pcol[:], 4, 1, ALU.arith_shift_right, ALU.bitwise_and, ["pcol"], ["pbit"])
+    tt(T.ind[:], T.srow[:], T.pbit[:], ALU.is_equal, ["srow", "pbit"], ["ind"])
+    op("v", lambda: g.vector.memset(T.ind0[:], 0.0), [], ["ind0"], vcost(4))
+    for h in range(2):
+        cp(T.ind0[64 * h:64 * h + 64, 2 * h:2 * h + 2], T.ind[64 * h:64 * h + 64, 0:2], ["ind", "ind0"], ["ind0"])
+
+    def sr(k, b, j):
+        return 24 * b + 3 * k + j
+
+    def wr(j, b):
+        return 8 * j + 4 * b
+
+    def stepped(k, b):
+        tt(T.wk[:, wr(k + 1, b) + 2, :], T.st[:, sr(k, b, 2), :], T.sg[:, 2 * k + b, :], ALU.mult,
+           [key("hf", k, b), key("sg", k, b)], [key("sh", k, b)])
+
     def probe(k, b):
-        i = 2 * k + b
-        tt(T.pk[:, i, 0:32], T.st[:, sti(k + 1, b) + 2, :], T.sg[:, i, :], ALU.mult,
-           [key("sm", k + 1, b), key("sg", k, b)], [key("sh", k, b)])
-        tt(T.w16[:, 2 + i, 0:32], T.st[:, sti(k, b), :], T.pk[:, i, 0:32], ALU.add,
-           [key("mb", k, b), key("sh", k, b)], [key("w", k + 1, b)])
+        w = wr(k + 1, b)
+        tt(T.wk[:, w:w + 2, :], T.st[:, sr(k, b, 1):sr(k, b, 3), :], T.wk[:, w + 2:w + 4, :], ALU.subtract,
+           [key("mb", k, b), key("hf", k, b), key("sh", k, b), key("dx", k, b)], [key("w", k + 1, b)])
 
     def half(k, b):
-        ts(T.st[:, sti(k + 1, b) + 2, :], T.st[:, sti(k, b) + 1, :], 1, 0xFFFE, ALU.arith_shift_right, ALU.bitwise_and,
-           [key("mb", k, b)], [key("sm", k + 1, b)])
-
-    def later(k, b):
-        i = 2 * k + b
-        if k < RO:
-            tt(T.pk[:, i, 32:64], T.dx[:, i, :], T.st[:, sti(k + 1, b) + 2, :], ALU.subtract,
-               [key("dx", k, b), key("sm", k + 1, b)], [key("db", k, b)])
-        else:
-            ts(T.mu[:, b, :], T.st[:, sti(k, b), :], C0, None, ALU.add, None, [key("mb", k, b)], [key("mu", 0, b)])
+        ts(T.st[:, sr(k, b, 2), :], T.st[:, sr(k, b, 0), :], 1, 0xFFFE, ALU.arith_shift_right, ALU.bitwise_and,
+           [key("mb", k, b)], [key("hf", k, b)])
 
     def rows(k, j):
-        return T.st[:, sti(k, 0) + j:sti(k, 1) + j + 1:3, :]
+        return T.st[:, sr(k, 0, j):sr(k, 1, j) + 1:24, :]
 
+    here[0] = -11.0
+    ts(T.t2[0:32, 0:2, :], T.n32[0:32, :], C0, None, ALU.subtract, None, ["n32"], both("t2", 0))
     for b in range(2):
-        cp(T.nn[:, b, :], T.n32[:, :, 16 * b:16 * b + 16], ["n32"], [key("nn", 0, b)])
-    NN = both("nn", 0)
+        mm(T.pg1[:, 32 * b:32 * b + 32], T.t2[0:32, b, :], T.idh[0:32, 0:32], True, True, [key("t2", 0, b), "idh"], ["pg1"])
+    NN = ["nn"]
+    ts(T.nn[:], T.pg1[:, 0:64], C0, None, ALU.add, None, ["pg1"], NN)
+    cp(T.wk[:, 0:5:4, :], T.pg1[:, 0:64], ["pg1"], both("w", 0))
     ts(T.tmp[:, 0:2, :], T.nn[:], 1, None, ALU.arith_shift_right, None, NN, ["m0"])
-    ts(T.w16[:, 0:2, 0:32], T.nn[:], C0, None, ALU.subtract, None, NN, both("w", 0))
-    ts(T.w16[:, 2:4, 0:32], T.tmp[:, 0:2, :], C0, None, ALU.subtract, None, ["m0"], both("w", 1))
-    for j in range(4):
-        mm(T.po[0:33, 128 * j:128 * j + 128], T.w16[:, j, 0:33], T.idh[:], True, True,
-           [key("w", j // 2, j % 2), "idh", "w16c"], ["po"])
-
-    def selo(i):
-        ts(T.selo[:, i, :], T.kk[:], float(128 * (i % 2) - 16 * (i // 2)), None, ALU.is_equal, None, ["kk"], ["selo%d" % i])
-    for i in range(4):
-        selo(i)
-    cp(T.t2[0:33, 0:4, :], T.po[0:33, :], ["po"], both("t2", 0) + both("t2", 1))
-    for i in range(4, 16):
-        selo(i)
+    ts(T.wk[:, 8:13:4, :], T.tmp[:, 0:2, :], C0, None, ALU.subtract, None, ["m0"], both("w", 1))
+    ts(T.tmp[:, 2:4, :], T.nn[:], 1, None, ALU.bitwise_and, None, NN, ["odd"])
+    ts(rows(0, 2), T.nn[:], 0xFFFE, None, ALU.bitwise_and, None, NN, both("hf", 0))
+    ts(rows(1, 1), T.tmp[:, 0:2, :], C0, None, ALU.subtract, None, ["m0"], ["m1"])
+    tt(rows(1, 0), T.nn[:], T.tmp[:, 2:4, :], ALU.add, NN + ["odd", "m1"], both("mb", 1))
+    ts(T.wk[:, 19:24:4, :], T.tmp[:, 2:4, :], 2.0, None, ALU.mult, None, ["odd"], both("dx", 1))
+    ts(T.sg[:, 2:4, :], T.tmp[:, 2:4, :], -1.0, 0.5, ALU.mult, ALU.add, ["odd"], both("sg", 1))
+    for b in range(2):
+        half(1, b)
+        stepped(1, b)
+        probe(1, b)
+    here[0] = -9.0
+    for h in range(2):
+        cp(T.ee[:, :, 32 * h:32 * h + 32], T.tmp[:, 2:4, :], ["odd"], ["ee%d" % h])
+    ts(T.g0[:, 0, :], T.tmp[:, 2:4, :], -KK, None, ALU.mult, None, ["odd"], ["ke"])
+    for h in range(2):
+        tt(T.cf[:, :, 32 * h:32 * h + 32], T.g0[:, 0, :], T.tmp[:, 0:2, :], ALU.add, ["ke", "m0"], ["cf%d" % h])
 
     def spread(buf, bank, j, b, c, h):
         for i in range(4):
             ch = 8 * c + 4 * h + i
             mm(buf[:, 128 * i:128 * i + 128], T.selt[0:33, ch, :], T.t2[0:33, 2 * j + b, :], True, True,
-               ["selt%d" % ch, key("t2", j, b)], [bank])
+               ["selt%d" % ch, "t2c", key("t2", j, b)], [bank])
 
-    def to_lists(buf, bank, c0, j, b, stop):
+    def turn(j, b):
+        mm(PG[b][0:32, 256:384], T.wk[:, wr(j, b), :], T.idh[:], True, True, [key("w", j, b), "idh"], ["pg%d" % b])
+
+    def turned(j, b):
+        cp(T.t2[0:32, 2 * j + b, :], PG[b][0:32, 256:384], ["pg%d" % b], [key("t2", j, b)])
+
+    def listed(buf, bank, j, b, start, stop):
         for a in range(8):
             for s in range(2):
-                mm(buf[:, c0 + a:c0 + 128:8], T.selo[:, 2 * a + s, :], T.w16[:, 2 * j + b, 16 * s:16 * s + 16], False,
-                   stop and a == 7 and s == 1, ["selo%d" % (2 * a + s), key("w", j, b)], [bank])
+                mm(buf[:, a:128:8], T.selo[:, 2 * a + s, :], T.wk[:, wr(j, b), 16 * s:16 * s + 16],
+                   start and a == 0 and s == 0, stop and a == 7 and s == 1, ["selo%d" % (2 * a + s), key("w", j, b)], [bank])
 
-    free = ((T.pa[:, 0:512], "pa0"), (T.pa[:, 512:1024], "pa1"), (T.pb0[:, 512:1024], "pb01"),
-            (T.pb1[:, 0:512], "pb10"), (T.pb1[:, 512:1024], "pb11"))
-
-    def lengths(hh):
-        buf, bank = free[hh % 5]
+    free = ((T.pa[:, 0:512], "pa0"), (T.pa[:, 512:1024], "pa1"), (T.pb0[:, 0:512], "pb00"), (T.pb0[:, 512:1024], "pb01"))
+    for hh in range(8):
+        buf, bank = free[hh % 4]
         spread(buf, bank, 0, hh // 4, (hh // 2) % 2, hh % 2)
-        act(T.nb[:, 512 * hh:512 * hh + 512], buf, ACT.Copy, [bank], ["nb%d" % hh])
+        act(T.nb[:, 512 * hh:512 * hh + 512], buf, ACT.Copy, [bank, "nb"], ["nb"])
 
-    first = ((T.pg, "pg"), (T.pb0, "pb00"))
-    for hh in range(5):
-        lengths(hh)
-    for j in range(2):
-        buf, bank = first[j]
-        mm(buf[:, 0:256], T.idh[:], T.zero[:], True, False, ["idh", "zero"], [bank])
+    here[0] = -11.0
+    waiting = ((T.pb1[:, 0:256], "pb10", True, False), (T.pb1[:, 256:512], "pb10", False, True), (T.pb1[:, 512:768], "pb11", True, True))
+    for j, (buf, bank, start, stop) in enumerate(waiting):
         for b in range(2):
-            to_lists(buf, bank, 128 * b, j, b, False)
-    for hh in range(5, 8):
-        lengths(hh)
-
-    ts(T.tmp[:, 2:4, :], T.nn[:], 1, None, ALU.bitwise_and, None, NN, ["odd"])
-    ts(rows(1, 2), T.nn[:], 0xFFFE, None, ALU.bitwise_and, None, NN, both("sm", 1))
-    ts(rows(1, 0), T.tmp[:, 0:2, :], C0, None, ALU.subtract, None, ["m0"], ["m1"])
-    tt(rows(1, 1), T.nn[:], T.tmp[:, 2:4, :], ALU.add, NN + ["odd", "m1"], both("mb", 1))
-    ts(T.dx[:, 2:4, :], T.tmp[:, 2:4, :], 2.0, None, ALU.mult, None, ["odd"], both("dx", 1))
-    ts(T.sg[:, 2:4, :], T.tmp[:, 2:4, :], 0.5, None, ALU.subtract, None, ["odd"], both("sg", 1))
-    ts(T.pbit[:], T.pcol[:], 4, 1, ALU.arith_shift_right, ALU.bitwise_and, ["pcol"], ["pbit"])
+            listed(buf[:, 128 * b:128 * b + 128], bank, j, b, start and b == 0, False)
     for b in range(2):
-        half(1, b)
-    cp(T.pflt[:], T.pbit[:], ["pbit"], ["pflt"])
-    for b in range(2):
-        probe(1, b)
-        later(1, b)
-    tt(T.ind[:], T.srow[:], T.pflt[:], ALU.is_equal, ["srow", "pflt"], ["ind"])
-
-    for i, x in enumerate(peers):
-        for s in range(2):
-            c = (2 * (r ^ x) + s) * 32
-            dma("s", T.lo32[:, c:c + 32], T.lld[i, 64 * s:64 * s + 64, :], [], ["lo32"], "lold", 128, [("larr", 8)])
-    for s, i in ((0, 0), (0, 1), (0, 2), (1, 1), (1, 0), (1, 2)):
-        row = 32 * (r ^ peers[i]) + 16 * s
-        dma("s", T.win[row:row + 16, :], T.wld[3 * s + i], [], ["win"], "winld", 112,
-            [("warr%d" % (3 * s + i), deal[s][i][1])])
-
-    ts(T.loc[:], T.lo32[:], C0, None, ALU.subtract, None, ["lo32"], ["loc"])
-    for q in range(N):
+        turn(2, b)
+        turned(2, b)
+    for q in [r] + [r ^ x for x in peers]:
         for a in range(8):
             for s in range(2):
-                c = (2 * q + s) * 32
-                mm(T.po[32 * q:32 * q + 32, a:256:8], T.selo[:, 2 * a + s, 32 * q:32 * q + 32], T.loc[:, c:c + 32],
-                   s == 0, s == 1, ["selo%d" % (2 * a + s), "loc"], ["po"])
-    cp(T.log[:], T.po[:, 0:256], ["po"], ["log"])
-    ts(T.off[:, 0:256], T.po[:, 0:256], C0, None, ALU.add, None, ["po"], both("off", 0))
-    for j in range(2):
-        buf, bank = first[j]
-        mm(buf[:, 0:256], T.idh[:], T.log[:], False, True, ["idh", "log"], [bank])
-        ts(T.off[:, 256 * (j + 1):256 * (j + 2)], buf[:, 0:256], 2 * C0, None, ALU.add, None, [bank], both("off", j + 1))
-
-    PB = (T.pb0, T.pb1)
+                src = T.los if q == r else T.loc
+                mm(T.pg1[32 * q:32 * q + 32, a:256:8], T.selo[:, 2 * a + s, 32 * q:32 * q + 32], src[:, 2 * q + s, :],
+                   s == 0, s == 1, ["selo%d" % (2 * a + s), "los0", "los1"], ["pg1"],
+                   pre=() if q == r else [("larr", 8)], at=0.0 if q == r else LANDS["lo"])
+    cp(T.log[:], T.pg1[:, 0:256], ["pg1"], ["log"])
+    ts(T.off[:, 0:256], T.pg1[:, 0:256], C0, None, ALU.add, None, ["pg1"], both("off", 0))
+    for buf, bank, start, stop in waiting:
+        mm(buf, T.idh[:], T.log[:], False, stop, ["idh", "log"], [bank])
+    ts(T.off[:, 256:768], T.pb1[:, 0:512], 2 * C0, None, ALU.add, None, ["pb10"], both("off", 1) + both("off", 2))
+    ts(T.off[:, 768:1024], T.pb1[:, 512:768], 2 * C0, None, ALU.add, None, ["pb11"], both("off", 3))
 
     def picked(slot, hh, k):
         c = 256 * slot + 32 * hh
         return T.win[:].indirect(T.off[:, c:c + 32 * k])
 
-    def gather(n, h):
-        hh = 2 * (n % 4) + h
-        act(T.xg[:, 512 * hh:512 * hh + 512], picked(n // 4 + 2, hh, 1), ACT.Copy,
-            ["win", key("off", n // 4 + 2, hh // 4)], ["x%d" % hh])
+    def gather(out, x, slot, c, h0, h1):
+        act(out[:, 1024 * c + 512 * h0:1024 * c + 512 * h1], picked(slot, 2 * c + h0, h1 - h0), ACT.Copy,
+            ["win", key("off", slot, c // 2)], names(x, c, h0, h1), True)
 
-    def gather0(n):
+    def lessened(out, x, slot, c, h0, h1):
+        sl = slice(1024 * c + 512 * h0, 1024 * c + 512 * h1)
+        tt(out[:, sl], picked(slot, 2 * c + h0, h1 - h0), T.s0[:, sl], ALU.subtract,
+           ["win", key("off", slot, c // 2)] + names("s", c, h0, h1), names(x, c, h0, h1))
+
+    def total(buf, c0, kd, c, j, ind=T.ind, name="ind", g0=0):
+        mm(PG[c // 2][:, g0 + 8 * (c % 2) + j:g0 + 64:16], buf[:, c0:c0 + 128], ind[:], True, True,
+           [kd, name], ["pg%d" % (c // 2)], True, join=True)
+
+    def ends(c):
+        for h0, h1 in (((0, 1), (1, 2)) if c == 0 else ((0, 2),)):
+            gather(T.s0, "s", 0, c, h0, h1)
+            lessened(T.rise, "r", 1, c, h0, h1)
+
+    def first(n, c):
+        (lessened if c in FIRST_ON_V else gather)(T.xz, "z", 2, c, 0, 2)
+        d = n % 3
         for h in range(2):
-            hh = 2 * n + h
-            act(T.s0[:, 512 * hh:512 * hh + 512], picked(0, hh, 1), ACT.Copy, ["win", key("off", 0, hh // 4)], ["s0%d" % hh])
+            sl = slice(1024 * c + 512 * h, 1024 * c + 512 * h + 512)
+            terms = [(BIG, "dia2", T.xz, "z"), (IDB, "dia0", T.xz, "z"), (NK, "dia4", T.rise, "r")]
+            if c not in FIRST_ON_V:
+                terms = [(NBIG, "dia3", T.s0, "s"), (NID, "dia1", T.s0, "s")] + terms
+            bank = "pb%d%d" % (n % 2, h)
+            for j, (m, km, x, kx) in enumerate(terms):
+                mm(PB[n % 2][:, 512 * h:512 * h + 512], m, x[:, sl], j == 0, j == len(terms) - 1,
+                   [km, "%s%d%d" % (kx, c, h)], [bank])
+            c0 = 1024 * d + 512 * h
+            act(T.dd[:, c0:c0 + 512], PB[n % 2][:, 512 * h:512 * h + 512], ACT.Abs, [bank], names("d", d, 4 * h, 4 * h + 4))
+            for j in range(4):
+                total(T.dd, c0 + 128 * j, "d%d%d" % (d, 4 * h + j), c, 4 * h + j, T.ind0, "ind0", 64)
 
-    def rise(n):
-        for hh, k in (((0, 1), (1, 1)) if n == 0 else ((2 * n, 2),)):
-            sl = slice(512 * hh, 512 * (hh + k))
-            tt(T.rise[:, sl], picked(1, hh, k), T.s0[:, sl], ALU.subtract,
-               ["win", key("off", 1, hh // 4)] + ["s0%d" % (hh + i) for i in range(k)], ["r%d" % (hh + i) for i in range(k)])
+    adds = [0]
 
-    def places(n):
+    def gain(n, e, c, cuts):
+        b, z = c // 2, c % 2
+        p, d = n % 2, n % 3
+        away = ADDED[e][c] if e in ADDED else ()
+        k0 = away[-1][1] if away else 0
+        col = 1024 * c
+
+        def banks(j0, j1):
+            return ["pb%d%d" % (p, h) for h in range(j0 // 4, (j1 + 3) // 4)]
         for h in range(2):
-            spread(PB[n % 2][:, 512 * h:512 * h + 512], "pb%d%d" % (n % 2, h), n // 4 + 1, (n % 4) // 2, n % 2, h)
-
-    def moved(n, h):
-        return n % 2 == 0 and h < OFF
-
-    def ycol(n):
-        return 2048 if n % 2 else 512 * (n % 4)
-
-    def lifted(n, h):
-        hh = 2 * (n % 4) + h
-        sl = slice(512 * hh, 512 * hh + 512)
-        m0, m1 = (T.idb, T.nid) if moved(n, h) else (T.nid, T.idb)
-        mm(T.pa[:, 512 * h:512 * h + 512], m0[:], T.s0[:, sl], True, False, ["nid", "idb", "s0%d" % hh], ["pa%d" % h])
-        mm(T.pa[:, 512 * h:512 * h + 512], m1[:], T.xg[:, sl], False, True, ["x%d" % hh], ["pa%d" % h])
-
-    adds = {}
-
-    def add(u):
-        sem = "acc%d" % (u // 512)
-        adds[sem] = adds.get(sem, 0) + 16
-        op("g", lambda: g.dma_start(T.yy[:, u:u + 512], T.uu[:, u:u + 512], accum_op=ALU.add), ["u%d" % u, "y%d" % u],
-           ["y%d" % u], sem, adds[sem])
-
-    def v1(n):
-        c = n % 4
-        y = ycol(n)
-        tt(T.yy[:, y:y + 1024], T.pa[:], T.nb[:, 1024 * c:1024 * c + 1024], ALU.mult,
-           ["pa0", "pa1", "nb%d" % (2 * c), "nb%d" % (2 * c + 1)], ["y%d" % y, "y%d" % (y + 512)])
+            step(e, b, "g%d%d" % (z, h))
+            gather(T.xg, "x", e + 2, c, h, h + 1)
         for h in range(2):
-            if moved(n, h):
-                add(y + 512 * h)
+            step(e, b, "t%d%d" % (z, h))
+            spread(T.pa[:, 512 * h:512 * h + 512], "pa%d" % h, e + 1, b, z, h)
+        for h in range(2):
+            sl = slice(col + 512 * h, col + 512 * h + 512)
+            bank = "pb%d%d" % (p, h)
+            step(e, b, "s%d%d" % (z, h))
+            mm(PB[p][:, 512 * h:512 * h + 512], IDB, T.s0[:, sl], True, False, ["dia0", "s%d%d" % (c, h)], [bank])
+            step(e, b, "l%d%d" % (z, h))
+            mm(PB[p][:, 512 * h:512 * h + 512], NID, T.xg[:, sl], False, True, ["dia1", "x%d%d" % (c, h)], [bank])
+        step(e, b, "u%d" % z)
+        tt(T.uu[:, col:col + 1024], T.pa[:], T.rise[:, col:col + 1024], ALU.mult,
+           ["pa0", "pa1", "r%d0" % c, "r%d1" % c], ["u%d" % c])
+        for h, (j0, j1) in enumerate(away):
+            step(e, b, "y%d%d" % (z, h))
+            sl = slice(col + 128 * j0, col + 128 * j1)
+            tt(T.yy[:, sl], PB[p][:, 128 * j0:128 * j1], T.nb[:, sl], ALU.mult, banks(j0, j1) + ["nb"], names("y", c, j0, j1))
+            k = adds[0]
+            adds[0] += 1
+            op("g", lambda sl=sl: g.dma_start(T.yy[:, sl], T.uu[:, sl], accum_op=ALU.add), ["u%d" % c] + names("y", c, j0, j1),
+               names("y", c, j0, j1), 1000.0, "acc%d" % (k % NACC), 16 * (k // NACC + 1),
+               late=LANDS["add"] + LANDS["add+"] * (j1 - j0))
+        if k0 < 8:
+            step(e, b, "y%d%d" % (z, len(away)))
+            src = PB[p][:, 128 * k0:1024]
+            tt(src, src, T.nb[:, col + 128 * k0:col + 1024], ALU.mult, banks(k0, 8) + ["nb"], banks(k0, 8))
+        runs = [(max(k0, j0), j1) for j0, j1 in cuts if j1 > k0]
+        for h, (j0, j1) in enumerate(runs):
+            step(e, b, "d%d%d" % (z, h))
+            tt(T.dd[:, 1024 * d + 128 * j0:1024 * d + 128 * j1], PB[p][:, 128 * j0:128 * j1],
+               T.uu[:, col + 128 * j0:col + 128 * j1], ALU.add, ["u%d" % c] + banks(j0, j1), names("d", d, j0, j1))
 
-    def v2(n):
-        c = n % 4
-        y = ycol(n)
-        k = OFF if n % 2 == 0 else 0
-        for h0, h1 in ((0, k), (k, 2)):
-            if h0 < h1:
-                banks = ["pb%d%d" % (n % 2, h) for h in range(h0, h1)]
-                src = PB[n % 2][:, 512 * h0:512 * h1]
-                away = moved(n, h0)
-                tt(T.uu[:, y + 512 * h0:y + 512 * h1] if away else src, src,
-                   T.rise[:, 1024 * c + 512 * h0:1024 * c + 512 * h1], ALU.mult,
-                   banks + ["r%d" % (2 * c + h) for h in range(h0, h1)],
-                   ["u%d" % (y + 512 * h) for h in range(h0, h1)] if away else banks)
+        def sums(buf, c0, x, i, j0, j1, name):
+            step(e, b, name)
+            act(buf[:, c0 + 128 * j0:c0 + 128 * j1], buf[:, c0 + 128 * j0:c0 + 128 * j1], ACT.Abs, names(x, i, j0, j1),
+                names(x, i, j0, j1))
+            step(e, b, "m" + name.lstrip("a"))
+            for j in range(j0, j1):
+                total(buf, c0 + 128 * j, "%s%d%d" % (x, i, j), c, j)
+        for h, (j0, j1) in enumerate((max(k0, j), j + 4) for j in (0, 4) if j + 4 > k0):
+            sums(T.dd, 1024 * d, "d", d, j0, j1, "a%d%d" % (z, h))
 
-    def v3(n, split):
-        p = n % 2
-        y = ycol(n)
-        k = OFF if p == 0 else 0
-        for h0, h1 in (((0, 1), (1, 2)) if split else ((k, 2),)):
-            if h0 < h1:
-                tt(T.dd[:, 1024 * p + 512 * h0:1024 * p + 512 * h1], PB[p][:, 512 * h0:512 * h1],
-                   T.yy[:, y + 512 * h0:y + 512 * h1], ALU.subtract,
-                   ["y%d" % (y + 512 * h) for h in range(h0, h1)] + ["pb%d%d" % (p, h) for h in range(h0, h1)],
-                   ["d%d%d" % (p, h) for h in range(h0, h1)])
-
-    def sizes(n, h):
-        if moved(n, h):
-            return T.yy, ycol(n) + 512 * h, "y%d" % (ycol(n) + 512 * h)
-        return T.dd, 1024 * (n % 2) + 512 * h, "d%d%d" % (n % 2, h)
-
-    def size(n, h):
-        buf, c, kd = sizes(n, h)
-        act(buf[:, c:c + 512], buf[:, c:c + 512], ACT.Abs, [kd], [kd])
-
-    def total(n, h):
-        b = (n % 4) // 2
-        buf, c, kd = sizes(n, h)
-        for i in range(4):
-            ch = 8 * (n % 2) + 4 * h + i
-            mm(T.pg[:, 64 * b + ch:64 * b + 64:16], buf[:, c + 128 * i:c + 128 * i + 128], T.ind[:], True, True,
-               [kd, "ind"], ["pg"])
+        def held():
+            for h, (j0, j1) in enumerate(away):
+                sums(T.yy, col, "y", c, j0, j1, "h%d" % h)
+        return held
 
     def decide(k, b):
         i = 2 * k + b
-        gw = T.pg[:, 64 * b:64 * b + 64]
+        bank = "pg%d" % b
+        gw = PG[b][:, 0:64]
         if k == 0:
-            cp(T.gm[:, 2 + b, :], gw, ["pg"], [key("gm", 1, b)])
-            return
-        if k == RO:
-            gw = T.pg[:, 64 * b:64 * b + 32]
-            tt(T.up[:, i, 0:32], gw, T.gm[:, i, 0:32], ALU.is_gt, ["pg", key("gm", k, b)], [key("up", k, b)])
-            tt(T.res[:, b, 2:4, :], gw, T.gm[:, i, 0:32], ALU.max, ["pg", key("gm", k, b)], [key("rg", 0, b)])
-            tt(T.dl[:, i, 0:32], T.up[:, i, 0:32], T.pk[:, i, 0:32], ALU.mult, [key("up", k, b), key("sh", k, b)], [key("dl", k, b)])
-            tt(T.res[:, b, 0:2, :], T.mu[:, b, :], T.dl[:, i, 0:32], ALU.add, [key("mu", 0, b), key("dl", k, b)], [key("rm", 0, b)])
-            send([(x, deal[b][j][0], deal[b][j][1], T.res[:, b, :, :], T.rld[:, 2 * j + b, :, :], "rarr%d" % j)
-                  for j, x in enumerate(peers)], [key("rg", 0, b), key("rm", 0, b)])
-            return
-        i1 = i + 2
-        tt(T.up[:, i, :], gw, T.gm[:, i, :], ALU.is_gt, ["pg", key("gm", k, b)], [key("up", k, b)])
-        tt(T.gm[:, i1, :], gw, T.gm[:, i, :], ALU.max, ["pg", key("gm", k, b)], [key("gm", k + 1, b)])
-        tt(T.dl[:, i, :], T.up[:, i, :], T.pk[:, i, :], ALU.mult,
-           [key("up", k, b), key("sh", k, b), key("db", k, b)], [key("dl", k, b)])
-        tt(T.st[:, sti(k + 1, b):sti(k + 1, b) + 2, :], T.st[:, sti(k, b):sti(k, b) + 3:2, :], T.dl[:, i, :], ALU.add,
-           [key("mb", k, b), key("sm", k, b), key("dl", k, b)], [key("mb", k + 1, b)])
-        tt(T.tau[:, i, :], T.dl[:, i, 0:32], T.sg[:, i, :], ALU.subtract, [key("dl", k, b), key("sg", k, b)], [key("tau", k, b)])
-        tt(T.dx[:, i1, :], T.st[:, sti(k + 1, b) + 1, :], T.st[:, sti(k + 1, b) + 2, :], ALU.subtract,
-           [key("mb", k + 1, b), key("sm", k + 1, b)], [key("dx", k + 1, b)])
-        half(k + 1, b)
-        tt(T.qq[:, i, :], T.dx[:, i1, :], T.tau[:, i, :], ALU.mult, [key("dx", k + 1, b), key("tau", k, b)], [key("qq", k, b)])
-        ts(T.sg[:, i1, :], T.qq[:, i, :], 0.0, 0.5, ALU.is_gt, ALU.subtract, [key("qq", k, b)], [key("sg", k + 1, b)])
-        probe(k + 1, b)
-
-    def lists(k, b):
-        if k < RO:
-            j = k + 2
-            mm(T.po[:, 0:128], T.idh[:], T.log[:, 128 * b:128 * b + 128], True, False, ["idh", "log"], ["po"])
-            to_lists(T.po, "po", 0, j, b, True)
-            mm(T.po[0:33, 128:256], T.w16[:, 2 * j + b, 0:33], T.idh[:], True, True, [key("w", j, b), "idh"], ["po"])
-
-    def publish(k, b, part):
-        if k < RO:
-            j = k + 2
-            c = 256 * (j + 1) + 128 * b
-            if part == 0:
-                ts(T.off[:, c:c + 128], T.po[:, 0:128], 2 * C0, None, ALU.add, None, ["po"], [key("off", j + 1, b)])
-            else:
-                cp(T.t2[0:33, 2 * j + b, :], T.po[0:33, 128:256], ["po"], [key("t2", j, b)])
-
-    def at(i, name, step, *args):
-        place[0] = (i, name)
-        step(*args)
-
-    def ahead(i, n):
-        if n < 4:
-            at(i, "gx0", gather0, n)
-        at(i, "gx0", gather, n, 0)
-        at(i, "gx1", gather, n, 1)
-        at(i, "px", places, n)
-        at(i, "lx0", lifted, n, 0)
-        at(i, "lx1", lifted, n, 1)
-        if n < 4:
-            at(i, "v2x", rise, n)
-        at(i, "v2x", v2, n)
-
-    slots = 2 * (RO + 1)
-    ahead(-1, 0)
-    for i in range(slots):
-        n0, n1 = 2 * i, 2 * i + 1
-        k, b = (i - 1) // 2, (i - 1) % 2
-        more = i + 1 < slots
-        at(i, "p1", places, n1)
-        at(i, "v1a", v1, n0)
-        if n1 < 4:
-            at(i, "g10", gather0, n1)
-        at(i, "g10", gather, n1, 0)
-        at(i, "g11", gather, n1, 1)
-        if n1 < 4:
-            at(i, "v2b", rise, n1)
-        at(i, "v2b", v2, n1)
-        at(i, "l10", lifted, n1, 0)
-        at(i, "l11", lifted, n1, 1)
-        if i > 0:
-            at(i, "dec", decide, k, b)
-            at(i, "lis", lists, k, b)
-            at(i, "pu0", publish, k, b, 0)
-            at(i, "pu1", publish, k, b, 1)
-            if 1 <= k < RO:
-                at(i, "lat", later, k + 1, b)
-        at(i, "v3a", v3, n0, False)
-        at(i, "v1b", v1, n1)
-        if more:
-            ahead(i, n1 + 1)
-        at(i, "v3b", v3, n1, SPLIT or not more)
-        for n, name in ((n0, "a"), (n1, "b")):
+            z = PG[b][:, 64:128]
+            ts(T.ci[:, b, :], z, 1.0 / KK, None, ALU.mult, None, [bank], [key("ci", 0, b)])
+            tt(T.g0[:, 2 + b, :], z, T.ee[:, b, :], ALU.mult, [bank, "ee0", "ee1"], [key("ez", 0, b)])
+            tt(T.g0[:, 4 + b, :], T.ci[:, b, :], T.cf[:, b, :], ALU.mult, [key("ci", 0, b), "cf0", "cf1"], [key("cz", 0, b)])
+            tt(T.g0[:, 4 + b, :], T.g0[:, 4 + b, :], T.g0[:, 2 + b, :], ALU.add, [key("ez", 0, b), key("cz", 0, b)], [key("cz", 0, b)])
             for h in range(2):
-                at(i, "s%s%d" % (name, h), size, n, h)
-                at(i, "t%s%d" % (name, h), total, n, h)
-    at(slots + 1, "dec", decide, RO, 1)
+                tt(T.gm[:, 2 + b, 32 * h:32 * h + 32], T.g0[:, 4 + b, 0:32], T.g0[:, 4 + b, 32:64], ALU.add,
+                   [key("cz", 0, b)], [key("gm%d" % h, 1, b)])
+            return
+        gk = [key("gm0", k, b), key("gm1", k, b)]
+        w = wr(k + 1, b)
+        up, dl = PG[b][:, 384:448], PG[b][:, 448:512]
+        step(k, b, "up")
+        if k == RO:
+            gw = PG[b][:, 0:32]
+            tt(up[:, 0:32], gw, T.gm[:, i, 0:32], ALU.is_gt, [bank] + gk, [key("up", k, b)])
+            tt(T.res[:, b, 32:64], gw, T.gm[:, i, 0:32], ALU.max, [bank] + gk, [key("rg", 0, b)])
+            tt(dl[:, 0:32], up[:, 0:32], T.wk[:, w + 2, :], ALU.mult, [bank, key("up", k, b), key("sh", k, b)], [key("dl", k, b)])
+            tt(T.res[:, b, 0:32], T.mu[:, b, :], dl[:, 0:32], ALU.subtract, [bank, key("mu", 0, b), key("dl", k, b)], [key("rm", 0, b)])
+            step(k, b, "lis")
+            for ph in range(2):
+                mm(PG[b][64 * ph:64 * ph + 64, 128:192], T.res[:, b, :], T.idf[:, 64 * ph:64 * ph + 64], True, True,
+                   [key("rg", 0, b), key("rm", 0, b), "idf"], [bank], True)
+            step(k, b, "off")
+            cp(T.rs[:, b, :], PG[b][:, 128:192], [bank], [key("rs", 0, b)])
+            send([(x, deal[b][j][0], deal[b][j][1], T.rs[:, b, :], T.rld[:, 2 * j + b, :], "rarr%d" % (2 * j + b))
+                  for j, x in enumerate(peers)], [key("rs", 0, b)], [key("gone", 0, b)], LANDS["res"] * (3 - 2 * b))
+            return
+        i1, w1 = i + 2, wr(k + 2, b)
+        tt(up, gw, T.gm[:, i, :], ALU.is_gt, [bank] + gk, [key("up", k, b)])
+        step(k, b, "dl")
+        tt(dl, up, T.wk[:, w + 1:w + 3, :], ALU.mult, [bank, key("up", k, b), key("sh", k, b), key("w", k + 1, b)], [key("dl", k, b)])
+        step(k, b, "st")
+        tt(T.st[:, sr(k + 1, b, 0):sr(k + 1, b, 2), :], T.st[:, sr(k - 1, b, 2):sr(k, b, 2):2, :], dl, ALU.subtract,
+           [bank, key("mb", k, b), key("hf", k - 1, b), key("dl", k, b)], [key("mb", k + 1, b)])
+        step(k, b, "tau")
+        tt(T.tau[:, i, :], dl[:, 32:64], T.sg[:, i, :], ALU.subtract, [bank, key("dl", k, b), key("sg", k, b)], [key("tau", k, b)])
+        step(k, b, "dx")
+        tt(T.wk[:, w1 + 3, :], T.st[:, sr(k + 1, b, 0), :], T.st[:, sr(k, b, 2), :], ALU.subtract,
+           [key("mb", k + 1, b), key("hf", k, b)], [key("dx", k + 1, b)])
+        step(k, b, "hf")
+        half(k + 1, b)
+        step(k, b, "qq")
+        tt(T.qq[:, i, :], T.wk[:, w1 + 3, :], T.tau[:, i, :], ALU.mult, [key("dx", k + 1, b), key("tau", k, b)], [key("qq", k, b)])
+        step(k, b, "gm")
+        tt(T.gm[:, i1, :], gw, T.gm[:, i, :], ALU.max, [bank] + gk, [key("gm0", k + 1, b), key("gm1", k + 1, b)])
+        step(k, b, "sg")
+        ts(T.sg[:, i1, :], T.qq[:, i, :], 0.0, 0.5, ALU.is_ge, ALU.subtract, [key("qq", k, b)], [key("sg", k + 1, b)])
+        step(k, b, "sh")
+        stepped(k + 1, b)
+        step(k, b, "w")
+        probe(k + 1, b)
+        step(k, b, "trn")
+        turn(k + 2, b)
+        step(k, b, "lis")
+        buf = PG[b][:, 128:256]
+        mm(buf, T.idh[:], T.log[:, 128 * b:128 * b + 128], True, False, ["idh", "log"], [bank])
+        listed(buf, bank, k + 2, b, False, True)
+        step(k, b, "off")
+        c = 256 * (k + 3) + 128 * b
+        ts(T.off[:, c:c + 128], buf, 2 * C0, None, ALU.add, None, [bank], [key("off", k + 3, b)])
+        step(k, b, "t2")
+        turned(k + 2, b)
+        if k + 1 == RO:
+            ts(T.mu[:, b, :], T.st[:, sr(RO, b, 1), :], C0, None, ALU.add, None, [key("mb", RO, b)], [key("mu", 0, b)])
 
-    RES = both("rg", 0) + both("rm", 0)
+    n = 0
+    for e in range(1, RO + 1):
+        for b in range(2):
+            held = []
+            for c in (2 * b, 2 * b + 1):
+                if e == 1:
+                    step(e, b, "end", 0.5 * (c % 2))
+                    ends(c)
+                    step(e, b, "fst", 0.5 * (c % 2))
+                    first(n, c)
+                    n += 1
+                    if c % 2:
+                        step(e, b, "fsum")
+                        decide(0, b)
+                held.append(gain(n, e, c, LAST if e == RO and c == 3 else RUNS[c % 2]))
+                n += 1
+            for sums in held:
+                sums()
+            decide(e, b)
+    here[:] = [99.0, None, None]
+
     outs = (T.ym, T.yg)
-    for t in range(2):
-        for s in range(2):
-            row = 32 * r + 16 * s
-            dma("s" if s == 0 else "a", outs[t][row:row + 16, :], T.res[:, :, 2 * t + s, :], RES, [], "outs", 256)
-    for i, x in enumerate(peers):
-        for t in range(2):
-            for s in range(2):
-                row = 32 * (r ^ x) + 16 * s
-                dma("s" if s == 0 else "a", outs[t][row:row + 16, :], T.rld[:, 2 * i:2 * i + 2, 2 * t + s, :], RES, [],
-                    "outs", 256, [("rarr%d" % i, deal[0][i][1] + deal[1][i][1])])
+    for b in range(2):
+        for i, x in enumerate((0,) + peers):
+            for ph in range(2):
+                for t in range(2):
+                    row, col, p0 = 32 * (r ^ x), 128 * b + 64 * ph, 64 * ph + 32 * t
+                    src = T.rld[p0:p0 + 32, 2 * i - 2 + b, :] if x else T.rs[p0:p0 + 32, b, :]
+                    dma("a" if b == 1 and ph == 1 else "s", outs[t][row:row + 32, col:col + 64], src,
+                        [key("gone" if x else "rs", 0, b)], [], "outs", 512,
+                        [("rarr%d" % (2 * i - 2 + b), deal[b][i - 1][1])] if x else ())
 
-    for i in arrange():
+    if not ORDER:
+        ORDER.extend(arrange(plan))
+    for i in ORDER:
         emit(plan[i])
     wait("g", "sent", sent[0])
     for q in cnt:

@@ -7,31 +7,42 @@ N = 4
 RO = 6
 C0 = 2048.0
 KK = 4096.0
-AWAY = ((0, 4), (4, 6))
-ADDED = {e: (AWAY, (), AWAY, ()) for e in range(1, RO)}
+AWAY = ((0, 4), (4, 7))
+WHOLE = ((0, 4), (4, 8))
+ADDED = {e: (AWAY, (), AWAY, ()) for e in range(2, RO)}
+ADDED[1] = (WHOLE, (), WHOLE, ())
+ADDED[RO] = (AWAY, (), (), ())
 RUNS = (((0, 8),), ((0, 4), (4, 8)))
-LAST = ((0, 4), (4, 8))
+LAST = ((0, 4), (4, 6), (6, 8))
 FIRST_ON_V = (1, 3)
 CYC, PE, GATHER, SEM, VFIX, AFIX = 0.83, 0.42, 1.56, 70.0, 40.0, 65.0
 LOOK = {"v": 150.0, "a": 150.0, "p": 150.0, "g": 0.0, "s": 0.0}
-LANDS = {"lo": 13000.0, "walk": 17000.0, "res": 3500.0, "add": 2000.0, "add+": 400.0}
-SWEEPS = 2
-FIXED = 99
-RANK = {"g00": 0.0, "g01": 0.0, "t00": 0.0, "t01": 0.0, "s00": 0.0, "s01": 0.0, "l00": 0.0, "l01": 0.0,
-        "u0": 0.0, "y00": 0.0, "y01": 0.0, "y02": 0.0, "d00": 0.0, "a00": 0.55, "a01": 0.55,
-        "g10": 0.5, "g11": 0.5, "t10": 0.5, "t11": 0.5, "s10": 0.5, "s11": 0.5, "l10": 0.5, "l11": 0.5,
-        "u1": 0.5, "y10": 0.5, "d10": 0.5, "d11": 0.5, "a10": 0.6, "a11": 0.6, "h0": 0.7, "h1": 0.7,
-        "m00": 0.55, "m01": 0.55, "m10": 0.6, "m11": 0.6, "mh0": 0.7, "mh1": 0.7,
-        "up": 0.8, "dl": 0.8, "st": 0.8, "tau": 0.8, "dx": 0.8, "hf": 0.8, "qq": 0.8, "gm": 0.8, "sg": 0.8, "sh": 0.8,
-        "w": 0.8, "trn": 0.8, "lis": 0.8, "off": 0.8, "t2": 0.8, "end": -0.74, "fst": 0.0, "fsum": 0.43}
+LANDS = {"lo": 12000.0, "walk": 14500.0, "res": 3500.0, "add": 2000.0, "add+": 400.0}
+SWEEPS = 1
+FIXED = 5
+RANK = {"g00": -0.78, "s01": -0.74, "s00": -0.72, "t00": -0.6, "l00": -0.59, "t01": -0.57, "g01": -0.52, "l01": -0.46,
+        "s10": -0.43, "d00": -0.38, "u0": -0.36, "y00": -0.33, "y01": -0.29, "g10": -0.26, "t10": -0.25, "u0b": -0.22,
+        "t11": -0.22, "l10": -0.16, "a00": -0.15, "s11": -0.05, "d10": -0.05, "u1": 0.04, "l11": 0.06, "g11": 0.14,
+        "m00": 0.18, "y10": 0.28, "d11": 0.29, "a01": 0.42, "ini": 0.49, "mh0": 0.49, "m10": 0.54, "h0": 0.61,
+        "m11": 0.62, "m01": 0.65, "mh1": 0.65, "a10": 0.66, "a11": 0.71, "h1": 0.71, "y11": 1.12,
+        "up": 0.79, "dl": 0.79, "gm": 0.82, "st": 0.83, "tau": 0.92, "dx": 0.97, "hf": 1.02, "trn": 1.03, "qq": 1.04,
+        "sg": 1.04, "sh": 1.04, "w": 1.04, "lis": 1.05, "off": 1.05, "gadd": 1.18, "t2": 1.19}
+START = {"s00": -1.26, "l11": -0.92, "e00": -0.89, "e10": -0.85, "t11": -0.82, "t00": -0.81, "t01": -0.79, "f10": -0.72,
+         "g00": -0.69, "e01": -0.63, "u0": -0.61, "f21": -0.49, "fsum": -0.49, "y00": -0.4, "m10": -0.37, "h0": -0.36,
+         "l01": -0.34, "f00": -0.31, "g01": -0.31, "l00": -0.29, "f20": -0.23, "s11": -0.23, "f11": -0.19, "g10": -0.1,
+         "y01": -0.03, "l10": 0.03, "e11": 0.06, "g11": 0.08, "t10": 0.11, "f30": 0.11, "f31": 0.16, "d10": 0.35,
+         "f01": 0.39, "a11": 0.42, "mh0": 0.43, "u1": 0.44, "d11": 0.45, "s01": 0.54, "m11": 0.58, "a10": 0.67,
+         "h1": 0.68, "mh1": 0.73, "y10": 1.51, "s10": 1.82}
+DECIDE = "gadd up dl st tau dx hf qq gm sg sh w trn lis off t2".split()
 
 SCRATCH = {
     "wst": ("dram", [6, 128, 512], "bfloat16"),
     "wld": ("dram", [6, 128, 512], "bfloat16"),
-    "los": ("sbuf", [128, 8, 32], "float16"),
-    "loc": ("sbuf", [128, 8, 32], "float16"),
+    "los": ("sbuf", [128, 16, 16], "float16"),
     "res": ("sbuf", [128, 2, 64], "float32"),
     "rs": ("sbuf", [128, 2, 64], "float32"),
+    "lst": ("dram", [4, 128, 64], "int32"),
+    "lld": ("dram", [3, 128, 64], "int32"),
     "rld": ("sbuf", [128, 6, 64], "float32"),
     "win": ("sbuf", [128, 4096], "bfloat16"),
     "xg": ("sbuf", [128, 4096], "bfloat16"),
@@ -52,6 +63,8 @@ SCRATCH = {
     "ind0": ("sbuf", [128, 4], "float32"),
     "dia": ("sbuf", [128, 5, 128], "bfloat16"),
     "idh": ("sbuf", [128, 128], "float16"),
+    "ndf": ("sbuf", [128, 128], "float32"),
+    "rl": ("sbuf", [128, 2, 64], "float32"),
     "idf": ("sbuf", [128, 128], "float32"),
     "selo": ("sbuf", [128, 16, 128], "float16"),
     "selt": ("sbuf", [128, 16, 128], "float16"),
@@ -81,7 +94,8 @@ SCRATCH = {
     "pg1": ("psum", [128, 512], "float32"),
 }
 NACC = 6
-SEMAPHORES = (["cv", "ca", "cp", "cg", "sent", "wstg0", "wstg1", "larr", "nld", "lold", "winld", "outs"]
+SEMAPHORES = (["cv", "ca", "cp", "cg", "sent", "wstg0", "wstg1", "larr", "nld", "lold", "winld", "outs", "accg0", "accg1",
+               "lstg"]
               + ["warr%d" % k for k in range(6)] + ["rarr%d" % k for k in range(6)] + ["acc%d" % k for k in range(NACC)])
 
 PSUM_KEYS = ("pa0", "pa1", "pb00", "pb01", "pb10", "pb11", "pg0", "pg1")
@@ -117,7 +131,7 @@ def arrange(plan):
             for k in o["writes"]:
                 before[i].update(wr.get(k, ()))
                 before[i].update(rd.get(k, ()))
-        if o["q"] in "gs" or o["sem"] is not None:
+        if (o["q"] in "gs" or o["sem"] is not None) and o["tag"] != "gadd":
             if o["q"] in last:
                 before[i].add(~last[o["q"]])
             last[o["q"]] = i
@@ -201,10 +215,11 @@ def rank_program(g, core, T, topo):
     def op(q, call, reads, writes, busy, sem=None, total=0, fresh=False, pre=(), late=0.0, at=0.0, join=False):
         plan.append(dict(q=q, call=call, reads=reads, writes=writes, sem=sem, total=total, fresh=fresh, pre=pre,
                          busy=busy, late=late, at=at, rank=here[0], join=join, slot=here[1], tag=here[2],
-                         fixed=here[1] is not None and here[0] >= FIXED))
+                         fixed=here[1] is not None and here[1] >= FIXED))
 
     def step(e, b, name, more=0.0):
-        here[:] = [2 * e + b + RANK[name] + more, 2 * e + b, name]
+        table = RANK if e > 1 or name in DECIDE else START
+        here[:] = [2 * e + b + table[name] + more, 2 * e + b, name]
 
     cnt = {"v": 0, "a": 0, "p": 0, "g": 0}
     seen = {q: {} for q in Q}
@@ -299,6 +314,8 @@ def rank_program(g, core, T, topo):
 
     peers = (3, 1, 2)
     deal = (((0, 4), (4, 2), (6, 2)), ((0, 2), (4, 4), (2, 2)))
+    back = ([[(j,) + deal[0][j] for j in range(3)]], (((0, 0, 4), (2, 4, 4)), ((1, 0, 8),)))
+    gets = [{j: ne for part in back[b] for j, e0, ne in part} for b in range(2)]
     PG = (T.pg0, T.pg1)
     PB = (T.pb0, T.pb1)
     IDB, NID, BIG, NBIG, NK = (T.dia[:, j, :] for j in range(5))
@@ -312,7 +329,8 @@ def rank_program(g, core, T, topo):
     def names(x, i, j0, j1):
         return ["%s%d%d" % (x, i, j) for j in range(j0, j1)]
 
-    dma("a", T.lo32[:], T.lo[:], [], ["lo32"], "lold", 16)
+    dma("a", T.lst[:], T.lo[:], [], ["lst"], "lstg", 16)
+    dma("a", T.lo32[32 * r:32 * r + 32, :], T.lo[32 * r:32 * r + 32, :], [], ["lo32"], "lold", 64)
     dma("a", T.n32[0:32, :], T.span[32 * r:32 * r + 32, :], [], ["n32"], "nld", 16)
     for s in range(2):
         for i, x in enumerate(peers):
@@ -330,19 +348,13 @@ def rank_program(g, core, T, topo):
 
     here[0] = -13.0
     ts(T.idh[:], T.jj[:], 0.0, None, ALU.is_equal, None, ["jj"], ["idh"])
-    ts(T.loh[:], T.lo32[:], C0, None, ALU.subtract, None, ["lo32"], ["loh"])
-    for b in range(2):
-        mm(T.pg0[:, 128 * b:128 * b + 128], T.loh[:, 128 * b:128 * b + 128], T.idh[:], True, True, ["loh", "idh"], ["pg0"])
-    for b in range(2):
-        cp(T.los[:, :, 16 * b:16 * b + 16], T.pg0[:, 128 * b:128 * b + 128], ["pg0"], ["los%d" % b])
-
-    def walks(s):
+    send([(x, deal[0][i][0], deal[0][i][1], T.lst[r ^ x], T.lld[i], "larr") for i, x in enumerate(peers)], ["lst"])
+    for s in range(2):
         send([(x, deal[s][i][0], deal[s][i][1], T.wst[3 * s + i], T.wld[3 * s + i], "warr%d" % (3 * s + i))
               for i, x in enumerate(peers)], ["wst%d" % s])
-    walks(0)
-    send([(x, deal[0][i][0], deal[0][i][1], T.los[:, 2 * (r ^ x):2 * (r ^ x) + 2, :], T.loc[:, 2 * r:2 * r + 2, :], "larr")
-          for i, x in enumerate(peers)], ["los0", "los1"])
-    walks(1)
+    for i, x in enumerate(peers):
+        dma("s", T.lo32[32 * (r ^ x):32 * (r ^ x) + 32, :], T.lld[i], [], ["lo32"], "lold", 64, [("larr", 8)],
+            LANDS["lo"] - 2000.0)
     for s, i in ((0, 0), (0, 1), (0, 2), (1, 1), (1, 0), (1, 2)):
         row = 32 * (r ^ peers[i]) + 16 * s
         dma("s", T.win[row:row + 16, :], T.wld[3 * s + i], [], ["win"], "winld", 112,
@@ -350,14 +362,17 @@ def rank_program(g, core, T, topo):
 
     here[0] = -12.0
     op("v", lambda: g.vector.memset(T.t2[32:33, :, :], C0), [], ["t2c"], vcost(1024))
-    for j, c in enumerate((1.0, -1.0, 2 * KK, -2 * KK, -KK)):
-        ts(T.dia[:, j, :], T.jj[:], 0.0, c, ALU.is_equal, ALU.mult, ["jj"], ["dia%d" % j])
-    for i in range(16):
-        ts(T.selo[:, i, :], T.kk[:], float(128 * (i % 2) - 16 * (i // 2)), None, ALU.is_equal, None, ["kk"], ["selo%d" % i])
-    here[0] = -10.0
+    ts(IDB, T.jj[:], 0.0, None, ALU.is_equal, None, ["jj"], ["dia0"])
     for c in range(16):
         ts(T.selt[0:33, c, :], T.kt[0:33, :], float(-c), T.dia[0:33, 0, 32:33], ALU.is_equal, ALU.max, ["kt", "dia0"],
            ["selt%d" % c])
+    here[0] = -11.0
+    for i in range(16):
+        ts(T.selo[:, i, :], T.kk[:], float(128 * (i % 2) - 16 * (i // 2)), None, ALU.is_equal, None, ["kk"], ["selo%d" % i])
+    here[0] = -10.0
+    for j, c in enumerate((-1.0, 2 * KK, -2 * KK, -KK)):
+        ts(T.dia[:, j + 1, :], T.jj[:], 0.0, c, ALU.is_equal, ALU.mult, ["jj"], ["dia%d" % (j + 1)])
+    ts(T.ndf[:], T.jj[:], 0.0, -1.0, ALU.is_equal, ALU.mult, ["jj"], ["ndf"])
     ts(T.idf[:], T.jj[:], 0.0, None, ALU.is_equal, None, ["jj"], ["idf"])
     ts(T.pbit[:], T.pcol[:], 4, 1, ALU.arith_shift_right, ALU.bitwise_and, ["pcol"], ["pbit"])
     tt(T.ind[:], T.srow[:], T.pbit[:], ALU.is_equal, ["srow", "pbit"], ["ind"])
@@ -387,11 +402,12 @@ def rank_program(g, core, T, topo):
     def rows(k, j):
         return T.st[:, sr(k, 0, j):sr(k, 1, j) + 1:24, :]
 
-    here[0] = -11.0
+    here[0] = -12.2
     ts(T.t2[0:32, 0:2, :], T.n32[0:32, :], C0, None, ALU.subtract, None, ["n32"], both("t2", 0))
     for b in range(2):
         mm(T.pg1[:, 32 * b:32 * b + 32], T.t2[0:32, b, :], T.idh[0:32, 0:32], True, True, [key("t2", 0, b), "idh"], ["pg1"])
     NN = ["nn"]
+    here[0] = -11.5
     ts(T.nn[:], T.pg1[:, 0:64], C0, None, ALU.add, None, ["pg1"], NN)
     cp(T.wk[:, 0:5:4, :], T.pg1[:, 0:64], ["pg1"], both("w", 0))
     ts(T.tmp[:, 0:2, :], T.nn[:], 1, None, ALU.arith_shift_right, None, NN, ["m0"])
@@ -432,10 +448,11 @@ def rank_program(g, core, T, topo):
                    start and a == 0 and s == 0, stop and a == 7 and s == 1, ["selo%d" % (2 * a + s), key("w", j, b)], [bank])
 
     free = ((T.pa[:, 0:512], "pa0"), (T.pa[:, 512:1024], "pa1"), (T.pb0[:, 0:512], "pb00"), (T.pb0[:, 512:1024], "pb01"))
+    here[0] = -12.5
     for hh in range(8):
         buf, bank = free[hh % 4]
         spread(buf, bank, 0, hh // 4, (hh // 2) % 2, hh % 2)
-        act(T.nb[:, 512 * hh:512 * hh + 512], buf, ACT.Copy, [bank, "nb"], ["nb"])
+        act(T.nb[:, 512 * hh:512 * hh + 512], buf, ACT.Copy, [bank], ["nb%d%d" % (hh // 2, hh % 2)])
 
     here[0] = -11.0
     waiting = ((T.pb1[:, 0:256], "pb10", True, False), (T.pb1[:, 256:512], "pb10", False, True), (T.pb1[:, 512:768], "pb11", True, True))
@@ -445,19 +462,21 @@ def rank_program(g, core, T, topo):
     for b in range(2):
         turn(2, b)
         turned(2, b)
-    for q in [r] + [r ^ x for x in peers]:
+    ts(T.loh[:], T.lo32[:], C0, None, ALU.subtract, None, ["lo32"], ["loh"])
+    for b in range(2):
+        mm(T.pg0[:, 128 * b:128 * b + 128], T.loh[:, 128 * b:128 * b + 128], T.idh[:], True, True, ["loh", "idh"], ["pg0"])
+    cp(T.los[:], T.pg0[:, 0:256], ["pg0"], ["los"])
+    for q in range(N):
         for a in range(8):
             for s in range(2):
-                src = T.los if q == r else T.loc
-                mm(T.pg1[32 * q:32 * q + 32, a:256:8], T.selo[:, 2 * a + s, 32 * q:32 * q + 32], src[:, 2 * q + s, :],
-                   s == 0, s == 1, ["selo%d" % (2 * a + s), "los0", "los1"], ["pg1"],
-                   pre=() if q == r else [("larr", 8)], at=0.0 if q == r else LANDS["lo"])
-    cp(T.log[:], T.pg1[:, 0:256], ["pg1"], ["log"])
+                mm(T.pg1[32 * q:32 * q + 32, a:256:8], T.selo[:, 2 * a + s, 32 * q:32 * q + 32], T.los[:, 2 * q + s:16:8, :],
+                   s == 0, s == 1, ["selo%d" % (2 * a + s), "los"], ["pg1"])
     ts(T.off[:, 0:256], T.pg1[:, 0:256], C0, None, ALU.add, None, ["pg1"], both("off", 0))
+    cp(T.log[:], T.pg1[:, 0:256], ["pg1"], ["log"])
     for buf, bank, start, stop in waiting:
         mm(buf, T.idh[:], T.log[:], False, stop, ["idh", "log"], [bank])
-    ts(T.off[:, 256:768], T.pb1[:, 0:512], 2 * C0, None, ALU.add, None, ["pb10"], both("off", 1) + both("off", 2))
-    ts(T.off[:, 768:1024], T.pb1[:, 512:768], 2 * C0, None, ALU.add, None, ["pb11"], both("off", 3))
+    for j in (0, 2, 1):
+        ts(T.off[:, 256 * j + 256:256 * j + 512], waiting[j][0], 2 * C0, None, ALU.add, None, [waiting[j][1]], both("off", j + 1))
 
     def picked(slot, hh, k):
         c = 256 * slot + 32 * hh
@@ -472,16 +491,27 @@ def rank_program(g, core, T, topo):
         tt(out[:, sl], picked(slot, 2 * c + h0, h1 - h0), T.s0[:, sl], ALU.subtract,
            ["win", key("off", slot, c // 2)] + names("s", c, h0, h1), names(x, c, h0, h1))
 
+    opened = [None, None]
+
     def total(buf, c0, kd, c, j, ind=T.ind, name="ind", g0=0):
-        mm(PG[c // 2][:, g0 + 8 * (c % 2) + j:g0 + 64:16], buf[:, c0:c0 + 128], ind[:], True, True,
-           [kd, name], ["pg%d" % (c // 2)], True, join=True)
+        out, left = PG[c // 2][:, g0 + 8 * (c % 2) + j:g0 + 64:16], opened[c // 2]
+
+        def call():
+            if left is None:
+                return g.tensor.matmul(out, buf[:, c0:c0 + 128], ind[:], True, True)
+            left[0] -= 1
+            return g.tensor.matmul(out, buf[:, c0:c0 + 128], ind[:], False, left[0] == 0)
+        op("p", call, [kd, name], ["pg%d" % (c // 2)], 10.0 + 256 * PE, join=True)
 
     def ends(c):
         for h0, h1 in (((0, 1), (1, 2)) if c == 0 else ((0, 2),)):
+            step(1, c // 2, "e0%d" % (c % 2))
             gather(T.s0, "s", 0, c, h0, h1)
+            step(1, c // 2, "e1%d" % (c % 2))
             lessened(T.rise, "r", 1, c, h0, h1)
 
     def first(n, c):
+        step(1, c // 2, "f0%d" % (c % 2))
         (lessened if c in FIRST_ON_V else gather)(T.xz, "z", 2, c, 0, 2)
         d = n % 3
         for h in range(2):
@@ -490,11 +520,14 @@ def rank_program(g, core, T, topo):
             if c not in FIRST_ON_V:
                 terms = [(NBIG, "dia3", T.s0, "s"), (NID, "dia1", T.s0, "s")] + terms
             bank = "pb%d%d" % (n % 2, h)
+            step(1, c // 2, "f1%d" % (c % 2))
             for j, (m, km, x, kx) in enumerate(terms):
                 mm(PB[n % 2][:, 512 * h:512 * h + 512], m, x[:, sl], j == 0, j == len(terms) - 1,
                    [km, "%s%d%d" % (kx, c, h)], [bank])
             c0 = 1024 * d + 512 * h
+            step(1, c // 2, "f2%d" % (c % 2))
             act(T.dd[:, c0:c0 + 512], PB[n % 2][:, 512 * h:512 * h + 512], ACT.Abs, [bank], names("d", d, 4 * h, 4 * h + 4))
+            step(1, c // 2, "f3%d" % (c % 2))
             for j in range(4):
                 total(T.dd, c0 + 128 * j, "d%d%d" % (d, 4 * h + j), c, 4 * h + j, T.ind0, "ind0", 64)
 
@@ -522,27 +555,42 @@ def rank_program(g, core, T, topo):
             mm(PB[p][:, 512 * h:512 * h + 512], IDB, T.s0[:, sl], True, False, ["dia0", "s%d%d" % (c, h)], [bank])
             step(e, b, "l%d%d" % (z, h))
             mm(PB[p][:, 512 * h:512 * h + 512], NID, T.xg[:, sl], False, True, ["dia1", "x%d%d" % (c, h)], [bank])
-        step(e, b, "u%d" % z)
-        tt(T.uu[:, col:col + 1024], T.pa[:], T.rise[:, col:col + 1024], ALU.mult,
-           ["pa0", "pa1", "r%d0" % c, "r%d1" % c], ["u%d" % c])
+        for h0, h1 in ((0, 1), (1, 2)) if away and e > 1 else ((0, 2),):
+            step(e, b, "u%db" % z if h0 else "u%d" % z)
+            sl = slice(col + 512 * h0, col + 512 * h1)
+            tt(T.uu[:, sl], T.pa[:, 512 * h0:512 * h1], T.rise[:, sl], ALU.mult,
+               ["pa%d" % h for h in range(h0, h1)] + names("r", c, h0, h1), names("u", c, h0, h1))
         for h, (j0, j1) in enumerate(away):
             step(e, b, "y%d%d" % (z, h))
-            sl = slice(col + 128 * j0, col + 128 * j1)
-            tt(T.yy[:, sl], PB[p][:, 128 * j0:128 * j1], T.nb[:, sl], ALU.mult, banks(j0, j1) + ["nb"], names("y", c, j0, j1))
+            sl = slice(col + 512 * h, col + 512 * h + 512)
+            tt(T.yy[:, sl], PB[p][:, 512 * h:512 * h + 512], T.nb[:, sl], ALU.mult, banks(j0, j1) + names("nb", c, h, h + 1),
+               names("y", c, 4 * h, 4 * h + 4))
             k = adds[0]
             adds[0] += 1
-            op("g", lambda sl=sl: g.dma_start(T.yy[:, sl], T.uu[:, sl], accum_op=ALU.add), ["u%d" % c] + names("y", c, j0, j1),
-               names("y", c, j0, j1), 1000.0, "acc%d" % (k % NACC), 16 * (k // NACC + 1),
-               late=LANDS["add"] + LANDS["add+"] * (j1 - j0))
-        if k0 < 8:
-            step(e, b, "y%d%d" % (z, len(away)))
-            src = PB[p][:, 128 * k0:1024]
-            tt(src, src, T.nb[:, col + 128 * k0:col + 1024], ALU.mult, banks(k0, 8) + ["nb"], banks(k0, 8))
-        runs = [(max(k0, j0), j1) for j0, j1 in cuts if j1 > k0]
+            sl = slice(col + 128 * j0, col + 128 * j1)
+            op("g", lambda sl=sl: g.dma_start(T.yy[:, sl], T.uu[:, sl], accum_op=ALU.add),
+               names("u", c, h, h + 1) + names("y", c, j0, j1), names("y", c, j0, j1), 1000.0, "acc%d" % (k % NACC),
+               16 * (k // NACC + 1), late=LANDS["add"] + LANDS["add+"] * (j1 - j0))
+        if 0 < k0 < 8:
+            step(e, b, "d00")
+            sl, sum_ = slice(col + 128 * k0, col + 1024), PB[p][:, 128 * k0:1024]
+            mm(sum_, T.idf[:], T.uu[:, sl], True, False, ["idf", "u%d1" % c], banks(k0, 8), True)
+            mm(sum_, T.idf[:], T.yy[:, sl], False, True, ["idf"] + names("y", c, k0, 8), banks(k0, 8), True)
+            step(e, b, "a00")
+            act(T.dd[:, 1024 * d + 128 * k0:1024 * d + 1024], sum_, ACT.Abs, banks(k0, 8), names("d", d, k0, 8))
+            step(e, b, "m00")
+            for j in range(k0, 8):
+                total(T.dd, 1024 * d + 128 * j, "d%d%d" % (d, j), c, j)
+        runs = () if away else cuts
+        for h, (j0, j1) in enumerate(() if away else WHOLE if len(cuts) > 2 else ((0, 8),)):
+            step(e, b, "y%d%d" % (z, h), 0.001 * h)
+            src = PB[p][:, 128 * j0:128 * j1]
+            tt(src, src, T.nb[:, col + 128 * j0:col + 128 * j1], ALU.mult, banks(j0, j1) + names("nb", c, 0, 2), banks(j0, j1))
         for h, (j0, j1) in enumerate(runs):
-            step(e, b, "d%d%d" % (z, h))
+            step(e, b, "d%d%d" % (z, min(h, 1)), 0.002 * h)
             tt(T.dd[:, 1024 * d + 128 * j0:1024 * d + 128 * j1], PB[p][:, 128 * j0:128 * j1],
-               T.uu[:, col + 128 * j0:col + 128 * j1], ALU.add, ["u%d" % c] + banks(j0, j1), names("d", d, j0, j1))
+               T.uu[:, col + 128 * j0:col + 128 * j1], ALU.add, names("u", c, j0 // 4, (j1 + 3) // 4) + banks(j0, j1),
+               names("d", d, j0, j1))
 
         def sums(buf, c0, x, i, j0, j1, name):
             step(e, b, name)
@@ -551,8 +599,8 @@ def rank_program(g, core, T, topo):
             step(e, b, "m" + name.lstrip("a"))
             for j in range(j0, j1):
                 total(buf, c0 + 128 * j, "%s%d%d" % (x, i, j), c, j)
-        for h, (j0, j1) in enumerate((max(k0, j), j + 4) for j in (0, 4) if j + 4 > k0):
-            sums(T.dd, 1024 * d, "d", d, j0, j1, "a%d%d" % (z, h))
+        for h, (j0, j1) in enumerate(WHOLE if len(runs) == 1 else runs):
+            sums(T.dd, 1024 * d, "d", d, j0, j1, "a%d%d" % (z, min(h, 1)))
 
         def held():
             for h, (j0, j1) in enumerate(away):
@@ -579,8 +627,8 @@ def rank_program(g, core, T, topo):
         step(k, b, "up")
         if k == RO:
             gw = PG[b][:, 0:32]
-            tt(up[:, 0:32], gw, T.gm[:, i, 0:32], ALU.is_gt, [bank] + gk, [key("up", k, b)])
-            tt(T.res[:, b, 32:64], gw, T.gm[:, i, 0:32], ALU.max, [bank] + gk, [key("rg", 0, b)])
+            tt(up[:, 0:32], gw, T.gm[:, 4 + b, 0:32], ALU.is_gt, [bank] + gk, [key("up", k, b)])
+            tt(T.res[:, b, 32:64], gw, T.gm[:, 4 + b, 0:32], ALU.max, [bank] + gk, [key("rg", 0, b)])
             tt(dl[:, 0:32], up[:, 0:32], T.wk[:, w + 2, :], ALU.mult, [bank, key("up", k, b), key("sh", k, b)], [key("dl", k, b)])
             tt(T.res[:, b, 0:32], T.mu[:, b, :], dl[:, 0:32], ALU.subtract, [bank, key("mu", 0, b), key("dl", k, b)], [key("rm", 0, b)])
             step(k, b, "lis")
@@ -589,11 +637,15 @@ def rank_program(g, core, T, topo):
                    [key("rg", 0, b), key("rm", 0, b), "idf"], [bank], True)
             step(k, b, "off")
             cp(T.rs[:, b, :], PG[b][:, 128:192], [bank], [key("rs", 0, b)])
-            send([(x, deal[b][j][0], deal[b][j][1], T.rs[:, b, :], T.rld[:, 2 * j + b, :], "rarr%d" % (2 * j + b))
-                  for j, x in enumerate(peers)], [key("rs", 0, b)], [key("gone", 0, b)], LANDS["res"] * (3 - 2 * b))
+            for part in back[b]:
+                send([(peers[j], e0, ne, T.rs[:, b, :], T.rld[:, 2 * j + b, :], "rarr%d" % (2 * j + b)) for j, e0, ne in part],
+                     [key("rs", 0, b)], [key("gone", 0, b)], LANDS["res"] * (3 - 2 * b))
             return
         i1, w1 = i + 2, wr(k + 2, b)
-        tt(up, gw, T.gm[:, i, :], ALU.is_gt, [bank] + gk, [key("up", k, b)])
+        if k == 1:
+            tt(up, gw, T.gm[:, i, :], ALU.is_gt, [bank] + gk, [key("up", k, b)])
+        else:
+            ts(up, gw, 0.0, None, ALU.is_gt, None, [bank], [key("up", k, b)])
         step(k, b, "dl")
         tt(dl, up, T.wk[:, w + 1:w + 3, :], ALU.mult, [bank, key("up", k, b), key("sh", k, b), key("w", k + 1, b)], [key("dl", k, b)])
         step(k, b, "st")
@@ -609,7 +661,14 @@ def rank_program(g, core, T, topo):
         step(k, b, "qq")
         tt(T.qq[:, i, :], T.wk[:, w1 + 3, :], T.tau[:, i, :], ALU.mult, [key("dx", k + 1, b), key("tau", k, b)], [key("qq", k, b)])
         step(k, b, "gm")
-        tt(T.gm[:, i1, :], gw, T.gm[:, i, :], ALU.max, [bank] + gk, [key("gm0", k + 1, b), key("gm1", k + 1, b)])
+        gn = [key("gm0", k + 1, b), key("gm1", k + 1, b)]
+        if k == 1:
+            tt(T.gm[:, i1, :], gw, T.gm[:, i, :], ALU.max, [bank] + gk, gn)
+        else:
+            act(T.rl[:, b, :], gw, ACT.Relu, [bank], ["rl%d" % b])
+            step(k, b, "gadd")
+            op("g", lambda: g.dma_start(T.gm[:, 4 + b, :], T.rl[:, b, :], accum_op=ALU.add), ["rl%d" % b] + gk, gn + gk,
+               1000.0, "accg%d" % b, 16 * (k - 1), late=LANDS["add"] + LANDS["add+"] * 0.5)
         step(k, b, "sg")
         ts(T.sg[:, i1, :], T.qq[:, i, :], 0.0, 0.5, ALU.is_ge, ALU.subtract, [key("qq", k, b)], [key("sg", k + 1, b)])
         step(k, b, "sh")
@@ -634,11 +693,15 @@ def rank_program(g, core, T, topo):
     for e in range(1, RO + 1):
         for b in range(2):
             held = []
+            opened[b] = None
+            if 1 < e < RO:
+                opened[b] = [16]
+                step(e, b, "ini")
+                mm(PG[b][:, 0:64], T.ndf[:], T.gm[:, 4 + b, :], True, False, ["ndf", key("gm0", e, b), key("gm1", e, b)],
+                   ["pg%d" % b], True)
             for c in (2 * b, 2 * b + 1):
                 if e == 1:
-                    step(e, b, "end", 0.5 * (c % 2))
                     ends(c)
-                    step(e, b, "fst", 0.5 * (c % 2))
                     first(n, c)
                     n += 1
                     if c % 2:
@@ -660,7 +723,7 @@ def rank_program(g, core, T, topo):
                     src = T.rld[p0:p0 + 32, 2 * i - 2 + b, :] if x else T.rs[p0:p0 + 32, b, :]
                     dma("a" if b == 1 and ph == 1 else "s", outs[t][row:row + 32, col:col + 64], src,
                         [key("gone" if x else "rs", 0, b)], [], "outs", 512,
-                        [("rarr%d" % (2 * i - 2 + b), deal[b][i - 1][1])] if x else ())
+                        [("rarr%d" % (2 * i - 2 + b), gets[b][i - 1])] if x else ())
 
     if not ORDER:
         ORDER.extend(arrange(plan))

from concourse.bass import DstId, RemoteDMATransfer
from concourse.mybir import AluOpType, ActivationFunctionType

ALU = AluOpType
ACT = ActivationFunctionType
N = 4
RO = 6
C0 = 2048.0
KK = 4096.0
AWAY = ((0, 4), (4, 7))
WHOLE = ((0, 4), (4, 8))
ADDED = {e: (AWAY, (), AWAY, ()) for e in range(2, RO)}
ADDED[1] = (WHOLE, (), WHOLE, ())
ADDED[RO] = (AWAY, (), (), ())
RUNS = (((0, 8),), ((0, 4), (4, 8)))
LAST = ((0, 4), (4, 6), (6, 8))
FIRST_ON_V = (1, 3)
CYC, PE, GATHER, SEM, VFIX, AFIX = 0.83, 0.42, 1.56, 70.0, 40.0, 65.0
LOOK = {"v": 150.0, "a": 150.0, "p": 150.0, "g": 0.0, "s": 0.0}
LANDS = {"lo": 12000.0, "walk": 14500.0, "res": 3500.0, "add": 2000.0, "add+": 400.0}
SWEEPS = 1
FIXED = 5
RANK = {"g00": -0.78, "s01": -0.74, "s00": -0.72, "t00": -0.6, "l00": -0.59, "t01": -0.57, "g01": -0.52, "l01": -0.46,
        "s10": -0.43, "d00": -0.38, "u0": -0.36, "y00": -0.33, "y01": -0.29, "g10": -0.26, "t10": -0.25, "u0b": -0.22,
        "t11": -0.22, "l10": -0.16, "a00": -0.15, "s11": -0.05, "d10": -0.05, "u1": 0.04, "l11": 0.06, "g11": 0.14,
        "m00": 0.18, "y10": 0.28, "d11": 0.29, "a01": 0.42, "ini": 0.49, "mh0": 0.49, "m10": 0.54, "h0": 0.61,
        "m11": 0.62, "m01": 0.65, "mh1": 0.65, "a10": 0.66, "a11": 0.71, "h1": 0.71, "y11": 1.12,
        "up": 0.79, "dl": 0.79, "gm": 0.82, "st": 0.83, "tau": 0.92, "dx": 0.97, "hf": 1.02, "trn": 1.03, "qq": 1.04,
        "sg": 1.04, "sh": 1.04, "w": 1.04, "lis": 1.05, "off": 1.05, "gadd": 1.18, "t2": 1.19}
START = {"s00": -1.26, "l11": -0.92, "e00": -0.89, "e10": -0.85, "t11": -0.82, "t00": -0.81, "t01": -0.79, "f10": -0.72,
         "g00": -0.69, "e01": -0.63, "u0": -0.61, "f21": -0.49, "fsum": -0.49, "y00": -0.4, "m10": -0.37, "h0": -0.36,
         "l01": -0.34, "f00": -0.31, "g01": -0.31, "l00": -0.29, "f20": -0.23, "s11": -0.23, "f11": -0.19, "g10": -0.1,
         "y01": -0.03, "l10": 0.03, "e11": 0.06, "g11": 0.08, "t10": 0.11, "f30": 0.11, "f31": 0.16, "d10": 0.35,
         "f01": 0.39, "a11": 0.42, "mh0": 0.43, "u1": 0.44, "d11": 0.45, "s01": 0.54, "m11": 0.58, "a10": 0.67,
         "h1": 0.68, "mh1": 0.73, "y10": 1.51, "s10": 1.82}
DECIDE = "gadd up dl st tau dx hf qq gm sg sh w trn lis off t2".split()

SCRATCH = {
    "wst": ("dram", [6, 128, 512], "bfloat16"),
    "wld": ("dram", [6, 128, 512], "bfloat16"),
    "los": ("sbuf", [128, 16, 16], "float16"),
    "res": ("sbuf", [128, 2, 64], "float32"),
    "rs": ("sbuf", [128, 2, 64], "float32"),
    "lst": ("dram", [4, 128, 64], "int32"),
    "lld": ("dram", [3, 128, 64], "int32"),
    "rld": ("sbuf", [128, 6, 64], "float32"),
    "win": ("sbuf", [128, 4096], "bfloat16"),
    "xg": ("sbuf", [128, 4096], "bfloat16"),
    "xz": ("sbuf", [128, 4096], "bfloat16"),
    "s0": ("sbuf", [128, 4096], "bfloat16"),
    "rise": ("sbuf", [128, 4096], "bfloat16"),
    "nb": ("sbuf", [128, 4096], "float32"),
    "yy": ("sbuf", [128, 4096], "float32"),
    "uu": ("sbuf", [128, 4096], "float32"),
    "dd": ("sbuf", [128, 3072], "float32"),
    "jj": ("sbuf", [128, 128], "bfloat16"),
    "kk": ("sbuf", [128, 128], "bfloat16"),
    "kt": ("sbuf", [128, 128], "bfloat16"),
    "pcol": ("sbuf", [128, 4], "int32"),
    "pbit": ("sbuf", [128, 4], "int32"),
    "srow": ("sbuf", [128, 4], "float32"),
    "ind": ("sbuf", [128, 4], "float32"),
    "ind0": ("sbuf", [128, 4], "float32"),
    "dia": ("sbuf", [128, 5, 128], "bfloat16"),
    "idh": ("sbuf", [128, 128], "float16"),
    "ndf": ("sbuf", [128, 128], "float32"),
    "rl": ("sbuf", [128, 2, 64], "float32"),
    "idf": ("sbuf", [128, 128], "float32"),
    "selo": ("sbuf", [128, 16, 128], "float16"),
    "selt": ("sbuf", [128, 16, 128], "float16"),
    "n32": ("sbuf", [128, 256], "int32"),
    "lo32": ("sbuf", [128, 256], "int32"),
    "loh": ("sbuf", [128, 256], "float16"),
    "log": ("sbuf", [128, 256], "float16"),
    "off": ("sbuf", [128, 9 * 256], "uint16"),
    "t2": ("sbuf", [128, 16, 128], "float16"),
    "nn": ("sbuf", [128, 2, 32], "int32"),
    "tmp": ("sbuf", [128, 4, 32], "int32"),
    "st": ("sbuf", [128, 48, 32], "int32"),
    "wk": ("sbuf", [128, 64, 32], "float16"),
    "sg": ("sbuf", [128, 16, 32], "float32"),
    "gm": ("sbuf", [128, 16, 64], "float32"),
    "tau": ("sbuf", [128, 16, 32], "float32"),
    "qq": ("sbuf", [128, 16, 32], "float32"),
    "mu": ("sbuf", [128, 2, 32], "float32"),
    "ee": ("sbuf", [128, 2, 64], "float32"),
    "cf": ("sbuf", [128, 2, 64], "float32"),
    "ci": ("sbuf", [128, 2, 64], "int32"),
    "g0": ("sbuf", [128, 6, 64], "float32"),
    "pa": ("psum", [128, 1024], "float32"),
    "pb0": ("psum", [128, 1024], "float32"),
    "pb1": ("psum", [128, 1024], "float32"),
    "pg0": ("psum", [128, 512], "float32"),
    "pg1": ("psum", [128, 512], "float32"),
}
NACC = 6
SEMAPHORES = (["cv", "ca", "cp", "cg", "sent", "wstg0", "wstg1", "larr", "nld", "lold", "winld", "outs", "accg0", "accg1",
               "lstg"]
              + ["warr%d" % k for k in range(6)] + ["rarr%d" % k for k in range(6)] + ["acc%d" % k for k in range(NACC)])

PSUM_KEYS = ("pa0", "pa1", "pb00", "pb01", "pb10", "pb11", "pg0", "pg1")
ORDER = []


def width(ap):
    n = 1
    for d in ap.shape[1:]:
        n *= d
    return n


def arrange(plan):
    n = len(plan)
    before = [set() for _ in range(n)]
    wr, rd, last, gate = {}, {}, {}, {}
    for i, o in enumerate(plan):
        for k in o["reads"]:
            before[i].update(wr.get(k, ()))
            if k in PSUM_KEYS:
                before[i].update(j for j in rd.get(k, ()) if plan[j]["q"] != o["q"])
        if o["join"]:
            k = o["writes"][0]
            if rd.get(k) or not plan[wr[k][-1]]["join"]:
                gate[k], wr[k], rd[k] = wr[k] + rd[k], [], []
            before[i].update(gate[k])
            wr[k].append(i)
            for k in o["reads"]:
                rd.setdefault(k, []).append(i)
            continue
        if not o["fresh"]:
            for k in o["writes"]:
                before[i].update(wr.get(k, ()))
                before[i].update(rd.get(k, ()))
        if (o["q"] in "gs" or o["sem"] is not None) and o["tag"] != "gadd":
            if o["q"] in last:
                before[i].add(~last[o["q"]])
            last[o["q"]] = i
        for k in o["reads"]:
            rd.setdefault(k, []).append(i)
        for k in o["writes"]:
            if o["fresh"]:
                wr.setdefault(k, []).append(i)
            else:
                wr[k] = [i]
                rd[k] = []
        before[i].discard(i)
    after = [[] for _ in range(n)]
    ahead = [[] for _ in range(n)]
    for i in range(n):
        for j in before[i]:
            gap = 0.0
            if j >= 0 and not (plan[i]["q"] == "p" == plan[j]["q"]):
                gap = plan[j]["late"] + SEM
            j = j if j >= 0 else ~j
            after[j].append((i, gap))
            ahead[i].append((j, gap))

    left = [len(x) for x in ahead]
    ready, last, links = [i for i in range(n) if left[i] == 0], {}, []
    while ready:
        i = min(ready, key=lambda i: (plan[i]["rank"], i))
        ready.remove(i)
        if plan[i]["fixed"]:
            if plan[i]["q"] in last:
                links.append((last[plan[i]["q"]], i))
            last[plan[i]["q"]] = i
        for j, gap in after[i]:
            left[j] -= 1
            if left[j] == 0:
                ready.append(j)
    for j, i in links:
        after[j].append((i, 0.0))
        ahead[i].append((j, 0.0))

    def sweep(nxt, prev, can, weight):
        left = [len(x) for x in prev]
        ready = {q: [] for q in LOOK}
        for i in range(n):
            if left[i] == 0:
                ready[plan[i]["q"]].append(i)
        free = {q: 0.0 for q in LOOK}
        out, end = [], [0.0] * n
        while len(out) < n:
            t, q = min((max(free[q], min(can[i] for i in ready[q])), q) for q in LOOK if ready[q])
            i = max((i for i in ready[q] if can[i] <= t + LOOK[q]), key=lambda i: (weight[i], -i))
            ready[q].remove(i)
            out.append(i)
            end[i] = free[q] = max(t, can[i]) + plan[i]["busy"]
            for j, gap in nxt[i]:
                can[j] = max(can[j], end[i] + gap)
                left[j] -= 1
                if left[j] == 0:
                    ready[plan[j]["q"]].append(j)
        return out, end

    weight = [-o["rank"] for o in plan]
    best = None
    for k in range(SWEEPS):
        out, end = sweep(after, ahead, [o["at"] for o in plan], weight)
        if best is None or max(end) < best[0]:
            best = (max(end), out)
        if k + 1 < SWEEPS:
            weight = sweep(ahead, after, [o["late"] for o in plan], end)[1]
    return best[1]


def rank_program(g, core, T, topo):
    r = T.rank_of(core)
    if r is None:
        return
    Q = {"v": g.vector, "a": g.scalar, "p": g.tensor, "g": g, "s": g.sync}
    plan = []
    here = [-9.0, None, None]

    def op(q, call, reads, writes, busy, sem=None, total=0, fresh=False, pre=(), late=0.0, at=0.0, join=False):
        plan.append(dict(q=q, call=call, reads=reads, writes=writes, sem=sem, total=total, fresh=fresh, pre=pre,
                         busy=busy, late=late, at=at, rank=here[0], join=join, slot=here[1], tag=here[2],
                         fixed=here[1] is not None and here[1] >= FIXED))

    def step(e, b, name, more=0.0):
        table = RANK if e > 1 or name in DECIDE else START
        here[:] = [2 * e + b + table[name] + more, 2 * e + b, name]

    cnt = {"v": 0, "a": 0, "p": 0, "g": 0}
    seen = {q: {} for q in Q}
    writer, readers, totals = {}, {}, {}

    def wait(q, sem, val):
        if seen[q].get(sem, 0) < val:
            Q[q].wait_ge(T.sem[sem], val)
            seen[q][sem] = val

    def emit(o):
        q = o["q"]
        own = "c" + q
        need = dict(o["pre"])

        def add(mark):
            if mark is not None and not (q == "p" and mark[0] == own):
                need[mark[0]] = max(need.get(mark[0], 0), mark[1])
        for k in o["reads"]:
            add(writer.get(k))
            if k in PSUM_KEYS:
                for s, v in readers.get(k, {}).items():
                    if s != own:
                        add((s, v))
        if not o["fresh"]:
            for k in o["writes"]:
                add(writer.get(k))
                for s, v in readers.get(k, {}).items():
                    add((s, v))
        for s in sorted(need):
            wait(q, s, need[s])
        made = o["call"]()
        if o["sem"] == "":
            return
        if o["sem"] is None:
            made.then_inc(T.sem[own], 1)
            cnt[q] += 1
            mark = (own, cnt[q])
        else:
            made.then_inc(T.sem[o["sem"]], 16)
            totals[o["sem"]] = o["total"]
            mark = (o["sem"], o["total"])
        if not o["fresh"]:
            for k in o["reads"]:
                readers.setdefault(k, {})[mark[0]] = mark[1]
        for k in o["writes"]:
            writer[k] = mark
            readers[k] = {}

    def dma(q, out, in_, reads, writes, sem, total, pre=(), at=0.0):
        op(q, lambda: Q[q].dma_start(out, in_), reads, writes, 60.0, sem, total, True, pre, 2000.0, at)

    def vcost(n):
        return VFIX + max(64.0, n) * CYC

    def tt(out, a, b, alu, reads, writes):
        n = width(out) * (1.0 if any(k in PSUM_KEYS for k in reads) else 2.0)
        op("v", lambda: g.vector.tensor_tensor(out, a, b, alu), reads, writes, vcost(n))

    def ts(out, a, s1, s2, o0, o1, reads, writes):
        n = width(out) / (2 if reads[0] in ("jj", "kk", "kt") else 1)
        if o1 is None:
            op("v", lambda: g.vector.tensor_scalar(out, a, s1, None, o0), reads, writes, vcost(n))
        else:
            op("v", lambda: g.vector.tensor_scalar(out, a, s1, s2, o0, o1), reads, writes, vcost(n))

    def cp(out, a, reads, writes):
        op("v", lambda: g.vector.tensor_copy(out, a), reads, writes, vcost(width(out)))

    def mm(out, lhsT, rhs, start, stop, reads, writes, wide=False, pre=(), at=0.0, join=False):
        c = 10.0 + max(min(64, width(lhsT)), width(rhs)) * (4 if wide else 1) * PE
        op("p", lambda: g.tensor.matmul(out, lhsT, rhs, start, stop), reads, writes, c, pre=pre, at=at, join=join)

    def act(out, a, func, reads, writes, gathered=False):
        op("a", lambda: g.scalar.activation(out, a, func), reads, writes,
           AFIX + width(out) * (GATHER if gathered else 1.0) * CYC)

    sent = [0]

    def send(parts, reads, writes=(), late=0.0):
        trs = []
        for x, e0, ne, src, dst, sem in parts:
            peer = T.cores[r ^ x]
            rid, pid, _ = topo.addr(peer)
            mask = 0
            for e in topo.engines(core, peer)[e0:e0 + ne]:
                mask |= 1 << e
            trs.append(RemoteDMATransfer(dst_ids=[DstId(rid=rid, pnc=pid)], dma_engine_mask=mask,
                                         remote_sem=T.sem[sem], src=src, dst=dst))
            sent[0] += ne
        op("g", lambda: g.remote_dma_fused(trs, local_sem=T.sem.sent), reads, list(writes), 700.0, "", late=late)

    peers = (3, 1, 2)
    deal = (((0, 4), (4, 2), (6, 2)), ((0, 2), (4, 4), (2, 2)))
    back = ([[(j,) + deal[0][j] for j in range(3)]], (((0, 0, 4), (2, 4, 4)), ((1, 0, 8),)))
    gets = [{j: ne for part in back[b] for j, e0, ne in part} for b in range(2)]
    PG = (T.pg0, T.pg1)
    PB = (T.pb0, T.pb1)
    IDB, NID, BIG, NBIG, NK = (T.dia[:, j, :] for j in range(5))

    def key(name, k, b):
        return "%s%d_%d" % (name, k, b)

    def both(name, k):
        return [key(name, k, 0), key(name, k, 1)]

    def names(x, i, j0, j1):
        return ["%s%d%d" % (x, i, j) for j in range(j0, j1)]

    dma("a", T.lst[:], T.lo[:], [], ["lst"], "lstg", 16)
    dma("a", T.lo32[32 * r:32 * r + 32, :], T.lo[32 * r:32 * r + 32, :], [], ["lo32"], "lold", 64)
    dma("a", T.n32[0:32, :], T.span[32 * r:32 * r + 32, :], [], ["n32"], "nld", 16)
    for s in range(2):
        for i, x in enumerate(peers):
            row = 32 * (r ^ x) + 16 * s
            dma("s", T.wst[3 * s + i], T.walk[row:row + 16, :], [], ["wst%d" % s], "wstg%d" % s, 48)
    dma("s", T.win[32 * r:32 * r + 32, :], T.walk[32 * r:32 * r + 32, :], [], ["win"], "winld", 112)

    def iota(out, pat, cm, name, **kw):
        op("g", lambda: g.iota(out, pat, 0, cm, **kw), [], [name], 130.0 + 2 * CYC * width(out))
    iota(T.jj[:], [[1, 128]], -1, "jj", allow_small_or_imprecise_dtypes=True)
    iota(T.kt[:], [[0, 4], [16, 2], [0, 16]], -1, "kt", allow_small_or_imprecise_dtypes=True)
    iota(T.kk[:], [[0, 4], [128, 2], [1, 16]], -1, "kk", allow_small_or_imprecise_dtypes=True)
    iota(T.pcol[:], [[0, 4]], 1, "pcol")
    iota(T.srow[:], [[0, 2], [1, 2]], 0, "srow", allow_small_or_imprecise_dtypes=True)

    here[0] = -13.0
    ts(T.idh[:], T.jj[:], 0.0, None, ALU.is_equal, None, ["jj"], ["idh"])
    send([(x, deal[0][i][0], deal[0][i][1], T.lst[r ^ x], T.lld[i], "larr") for i, x in enumerate(peers)], ["lst"])
    for s in range(2):
        send([(x, deal[s][i][0], deal[s][i][1], T.wst[3 * s + i], T.wld[3 * s + i], "warr%d" % (3 * s + i))
              for i, x in enumerate(peers)], ["wst%d" % s])
    for i, x in enumerate(peers):
        dma("s", T.lo32[32 * (r ^ x):32 * (r ^ x) + 32, :], T.lld[i], [], ["lo32"], "lold", 64, [("larr", 8)],
            LANDS["lo"] - 2000.0)
    for s, i in ((0, 0), (0, 1), (0, 2), (1, 1), (1, 0), (1, 2)):
        row = 32 * (r ^ peers[i]) + 16 * s
        dma("s", T.win[row:row + 16, :], T.wld[3 * s + i], [], ["win"], "winld", 112,
            [("warr%d" % (3 * s + i), deal[s][i][1])], LANDS["walk"] - 2000.0)

    here[0] = -12.0
    op("v", lambda: g.vector.memset(T.t2[32:33, :, :], C0), [], ["t2c"], vcost(1024))
    ts(IDB, T.jj[:], 0.0, None, ALU.is_equal, None, ["jj"], ["dia0"])
    for c in range(16):
        ts(T.selt[0:33, c, :], T.kt[0:33, :], float(-c), T.dia[0:33, 0, 32:33], ALU.is_equal, ALU.max, ["kt", "dia0"],
           ["selt%d" % c])
    here[0] = -11.0
    for i in range(16):
        ts(T.selo[:, i, :], T.kk[:], float(128 * (i % 2) - 16 * (i // 2)), None, ALU.is_equal, None, ["kk"], ["selo%d" % i])
    here[0] = -10.0
    for j, c in enumerate((-1.0, 2 * KK, -2 * KK, -KK)):
        ts(T.dia[:, j + 1, :], T.jj[:], 0.0, c, ALU.is_equal, ALU.mult, ["jj"], ["dia%d" % (j + 1)])
    ts(T.ndf[:], T.jj[:], 0.0, -1.0, ALU.is_equal, ALU.mult, ["jj"], ["ndf"])
    ts(T.idf[:], T.jj[:], 0.0, None, ALU.is_equal, None, ["jj"], ["idf"])
    ts(T.pbit[:], T.pcol[:], 4, 1, ALU.arith_shift_right, ALU.bitwise_and, ["pcol"], ["pbit"])
    tt(T.ind[:], T.srow[:], T.pbit[:], ALU.is_equal, ["srow", "pbit"], ["ind"])
    op("v", lambda: g.vector.memset(T.ind0[:], 0.0), [], ["ind0"], vcost(4))
    for h in range(2):
        cp(T.ind0[64 * h:64 * h + 64, 2 * h:2 * h + 2], T.ind[64 * h:64 * h + 64, 0:2], ["ind", "ind0"], ["ind0"])

    def sr(k, b, j):
        return 24 * b + 3 * k + j

    def wr(j, b):
        return 8 * j + 4 * b

    def stepped(k, b):
        tt(T.wk[:, wr(k + 1, b) + 2, :], T.st[:, sr(k, b, 2), :], T.sg[:, 2 * k + b, :], ALU.mult,
           [key("hf", k, b), key("sg", k, b)], [key("sh", k, b)])

    def probe(k, b):
        w = wr(k + 1, b)
        tt(T.wk[:, w:w + 2, :], T.st[:, sr(k, b, 1):sr(k, b, 3), :], T.wk[:, w + 2:w + 4, :], ALU.subtract,
           [key("mb", k, b), key("hf", k, b), key("sh", k, b), key("dx", k, b)], [key("w", k + 1, b)])

    def half(k, b):
        ts(T.st[:, sr(k, b, 2), :], T.st[:, sr(k, b, 0), :], 1, 0xFFFE, ALU.arith_shift_right, ALU.bitwise_and,
           [key("mb", k, b)], [key("hf", k, b)])

    def rows(k, j):
        return T.st[:, sr(k, 0, j):sr(k, 1, j) + 1:24, :]

    here[0] = -12.2
    ts(T.t2[0:32, 0:2, :], T.n32[0:32, :], C0, None, ALU.subtract, None, ["n32"], both("t2", 0))
    for b in range(2):
        mm(T.pg1[:, 32 * b:32 * b + 32], T.t2[0:32, b, :], T.idh[0:32, 0:32], True, True, [key("t2", 0, b), "idh"], ["pg1"])
    NN = ["nn"]
    here[0] = -11.5
    ts(T.nn[:], T.pg1[:, 0:64], C0, None, ALU.add, None, ["pg1"], NN)
    cp(T.wk[:, 0:5:4, :], T.pg1[:, 0:64], ["pg1"], both("w", 0))
    ts(T.tmp[:, 0:2, :], T.nn[:], 1, None, ALU.arith_shift_right, None, NN, ["m0"])
    ts(T.wk[:, 8:13:4, :], T.tmp[:, 0:2, :], C0, None, ALU.subtract, None, ["m0"], both("w", 1))
    ts(T.tmp[:, 2:4, :], T.nn[:], 1, None, ALU.bitwise_and, None, NN, ["odd"])
    ts(rows(0, 2), T.nn[:], 0xFFFE, None, ALU.bitwise_and, None, NN, both("hf", 0))
    ts(rows(1, 1), T.tmp[:, 0:2, :], C0, None, ALU.subtract, None, ["m0"], ["m1"])
    tt(rows(1, 0), T.nn[:], T.tmp[:, 2:4, :], ALU.add, NN + ["odd", "m1"], both("mb", 1))
    ts(T.wk[:, 19:24:4, :], T.tmp[:, 2:4, :], 2.0, None, ALU.mult, None, ["odd"], both("dx", 1))
    ts(T.sg[:, 2:4, :], T.tmp[:, 2:4, :], -1.0, 0.5, ALU.mult, ALU.add, ["odd"], both("sg", 1))
    for b in range(2):
        half(1, b)
        stepped(1, b)
        probe(1, b)
    here[0] = -9.0
    for h in range(2):
        cp(T.ee[:, :, 32 * h:32 * h + 32], T.tmp[:, 2:4, :], ["odd"], ["ee%d" % h])
    ts(T.g0[:, 0, :], T.tmp[:, 2:4, :], -KK, None, ALU.mult, None, ["odd"], ["ke"])
    for h in range(2):
        tt(T.cf[:, :, 32 * h:32 * h + 32], T.g0[:, 0, :], T.tmp[:, 0:2, :], ALU.add, ["ke", "m0"], ["cf%d" % h])

    def spread(buf, bank, j, b, c, h):
        for i in range(4):
            ch = 8 * c + 4 * h + i
            mm(buf[:, 128 * i:128 * i + 128], T.selt[0:33, ch, :], T.t2[0:33, 2 * j + b, :], True, True,
               ["selt%d" % ch, "t2c", key("t2", j, b)], [bank])

    def turn(j, b):
        mm(PG[b][0:32, 256:384], T.wk[:, wr(j, b), :], T.idh[:], True, True, [key("w", j, b), "idh"], ["pg%d" % b])

    def turned(j, b):
        cp(T.t2[0:32, 2 * j + b, :], PG[b][0:32, 256:384], ["pg%d" % b], [key("t2", j, b)])

    def listed(buf, bank, j, b, start, stop):
        for a in range(8):
            for s in range(2):
                mm(buf[:, a:128:8], T.selo[:, 2 * a + s, :], T.wk[:, wr(j, b), 16 * s:16 * s + 16],
                   start and a == 0 and s == 0, stop and a == 7 and s == 1, ["selo%d" % (2 * a + s), key("w", j, b)], [bank])

    free = ((T.pa[:, 0:512], "pa0"), (T.pa[:, 512:1024], "pa1"), (T.pb0[:, 0:512], "pb00"), (T.pb0[:, 512:1024], "pb01"))
    here[0] = -12.5
    for hh in range(8):
        buf, bank = free[hh % 4]
        spread(buf, bank, 0, hh // 4, (hh // 2) % 2, hh % 2)
        act(T.nb[:, 512 * hh:512 * hh + 512], buf, ACT.Copy, [bank], ["nb%d%d" % (hh // 2, hh % 2)])

    here[0] = -11.0
    waiting = ((T.pb1[:, 0:256], "pb10", True, False), (T.pb1[:, 256:512], "pb10", False, True), (T.pb1[:, 512:768], "pb11", True, True))
    for j, (buf, bank, start, stop) in enumerate(waiting):
        for b in range(2):
            listed(buf[:, 128 * b:128 * b + 128], bank, j, b, start and b == 0, False)
    for b in range(2):
        turn(2, b)
        turned(2, b)
    ts(T.loh[:], T.lo32[:], C0, None, ALU.subtract, None, ["lo32"], ["loh"])
    for b in range(2):
        mm(T.pg0[:, 128 * b:128 * b + 128], T.loh[:, 128 * b:128 * b + 128], T.idh[:], True, True, ["loh", "idh"], ["pg0"])
    cp(T.los[:], T.pg0[:, 0:256], ["pg0"], ["los"])
    for q in range(N):
        for a in range(8):
            for s in range(2):
                mm(T.pg1[32 * q:32 * q + 32, a:256:8], T.selo[:, 2 * a + s, 32 * q:32 * q + 32], T.los[:, 2 * q + s:16:8, :],
                   s == 0, s == 1, ["selo%d" % (2 * a + s), "los"], ["pg1"])
    ts(T.off[:, 0:256], T.pg1[:, 0:256], C0, None, ALU.add, None, ["pg1"], both("off", 0))
    cp(T.log[:], T.pg1[:, 0:256], ["pg1"], ["log"])
    for buf, bank, start, stop in waiting:
        mm(buf, T.idh[:], T.log[:], False, stop, ["idh", "log"], [bank])
    for j in (0, 2, 1):
        ts(T.off[:, 256 * j + 256:256 * j + 512], waiting[j][0], 2 * C0, None, ALU.add, None, [waiting[j][1]], both("off", j + 1))

    def picked(slot, hh, k):
        c = 256 * slot + 32 * hh
        return T.win[:].indirect(T.off[:, c:c + 32 * k])

    def gather(out, x, slot, c, h0, h1):
        act(out[:, 1024 * c + 512 * h0:1024 * c + 512 * h1], picked(slot, 2 * c + h0, h1 - h0), ACT.Copy,
            ["win", key("off", slot, c // 2)], names(x, c, h0, h1), True)

    def lessened(out, x, slot, c, h0, h1):
        sl = slice(1024 * c + 512 * h0, 1024 * c + 512 * h1)
        tt(out[:, sl], picked(slot, 2 * c + h0, h1 - h0), T.s0[:, sl], ALU.subtract,
           ["win", key("off", slot, c // 2)] + names("s", c, h0, h1), names(x, c, h0, h1))

    opened = [None, None]

    def total(buf, c0, kd, c, j, ind=T.ind, name="ind", g0=0):
        out, left = PG[c // 2][:, g0 + 8 * (c % 2) + j:g0 + 64:16], opened[c // 2]

        def call():
            if left is None:
                return g.tensor.matmul(out, buf[:, c0:c0 + 128], ind[:], True, True)
            left[0] -= 1
            return g.tensor.matmul(out, buf[:, c0:c0 + 128], ind[:], False, left[0] == 0)
        op("p", call, [kd, name], ["pg%d" % (c // 2)], 10.0 + 256 * PE, join=True)

    def ends(c):
        for h0, h1 in (((0, 1), (1, 2)) if c == 0 else ((0, 2),)):
            step(1, c // 2, "e0%d" % (c % 2))
            gather(T.s0, "s", 0, c, h0, h1)
            step(1, c // 2, "e1%d" % (c % 2))
            lessened(T.rise, "r", 1, c, h0, h1)

    def first(n, c):
        step(1, c // 2, "f0%d" % (c % 2))
        (lessened if c in FIRST_ON_V else gather)(T.xz, "z", 2, c, 0, 2)
        d = n % 3
        for h in range(2):
            sl = slice(1024 * c + 512 * h, 1024 * c + 512 * h + 512)
            terms = [(BIG, "dia2", T.xz, "z"), (IDB, "dia0", T.xz, "z"), (NK, "dia4", T.rise, "r")]
            if c not in FIRST_ON_V:
                terms = [(NBIG, "dia3", T.s0, "s"), (NID, "dia1", T.s0, "s")] + terms
            bank = "pb%d%d" % (n % 2, h)
            step(1, c // 2, "f1%d" % (c % 2))
            for j, (m, km, x, kx) in enumerate(terms):
                mm(PB[n % 2][:, 512 * h:512 * h + 512], m, x[:, sl], j == 0, j == len(terms) - 1,
                   [km, "%s%d%d" % (kx, c, h)], [bank])
            c0 = 1024 * d + 512 * h
            step(1, c // 2, "f2%d" % (c % 2))
            act(T.dd[:, c0:c0 + 512], PB[n % 2][:, 512 * h:512 * h + 512], ACT.Abs, [bank], names("d", d, 4 * h, 4 * h + 4))
            step(1, c // 2, "f3%d" % (c % 2))
            for j in range(4):
                total(T.dd, c0 + 128 * j, "d%d%d" % (d, 4 * h + j), c, 4 * h + j, T.ind0, "ind0", 64)

    adds = [0]

    def gain(n, e, c, cuts):
        b, z = c // 2, c % 2
        p, d = n % 2, n % 3
        away = ADDED[e][c] if e in ADDED else ()
        k0 = away[-1][1] if away else 0
        col = 1024 * c

        def banks(j0, j1):
            return ["pb%d%d" % (p, h) for h in range(j0 // 4, (j1 + 3) // 4)]
        for h in range(2):
            step(e, b, "g%d%d" % (z, h))
            gather(T.xg, "x", e + 2, c, h, h + 1)
        for h in range(2):
            step(e, b, "t%d%d" % (z, h))
            spread(T.pa[:, 512 * h:512 * h + 512], "pa%d" % h, e + 1, b, z, h)
        for h in range(2):
            sl = slice(col + 512 * h, col + 512 * h + 512)
            bank = "pb%d%d" % (p, h)
            step(e, b, "s%d%d" % (z, h))
            mm(PB[p][:, 512 * h:512 * h + 512], IDB, T.s0[:, sl], True, False, ["dia0", "s%d%d" % (c, h)], [bank])
            step(e, b, "l%d%d" % (z, h))
            mm(PB[p][:, 512 * h:512 * h + 512], NID, T.xg[:, sl], False, True, ["dia1", "x%d%d" % (c, h)], [bank])
        for h0, h1 in ((0, 1), (1, 2)) if away and e > 1 else ((0, 2),):
            step(e, b, "u%db" % z if h0 else "u%d" % z)
            sl = slice(col + 512 * h0, col + 512 * h1)
            tt(T.uu[:, sl], T.pa[:, 512 * h0:512 * h1], T.rise[:, sl], ALU.mult,
               ["pa%d" % h for h in range(h0, h1)] + names("r", c, h0, h1), names("u", c, h0, h1))
        for h, (j0, j1) in enumerate(away):
            step(e, b, "y%d%d" % (z, h))
            sl = slice(col + 512 * h, col + 512 * h + 512)
            tt(T.yy[:, sl], PB[p][:, 512 * h:512 * h + 512], T.nb[:, sl], ALU.mult, banks(j0, j1) + names("nb", c, h, h + 1),
               names("y", c, 4 * h, 4 * h + 4))
            k = adds[0]
            adds[0] += 1
            sl = slice(col + 128 * j0, col + 128 * j1)
            op("g", lambda sl=sl: g.dma_start(T.yy[:, sl], T.uu[:, sl], accum_op=ALU.add),
               names("u", c, h, h + 1) + names("y", c, j0, j1), names("y", c, j0, j1), 1000.0, "acc%d" % (k % NACC),
               16 * (k // NACC + 1), late=LANDS["add"] + LANDS["add+"] * (j1 - j0))
        if 0 < k0 < 8:
            step(e, b, "d00")
            sl, sum_ = slice(col + 128 * k0, col + 1024), PB[p][:, 128 * k0:1024]
            mm(sum_, T.idf[:], T.uu[:, sl], True, False, ["idf", "u%d1" % c], banks(k0, 8), True)
            mm(sum_, T.idf[:], T.yy[:, sl], False, True, ["idf"] + names("y", c, k0, 8), banks(k0, 8), True)
            step(e, b, "a00")
            act(T.dd[:, 1024 * d + 128 * k0:1024 * d + 1024], sum_, ACT.Abs, banks(k0, 8), names("d", d, k0, 8))
            step(e, b, "m00")
            for j in range(k0, 8):
                total(T.dd, 1024 * d + 128 * j, "d%d%d" % (d, j), c, j)
        runs = () if away else cuts
        for h, (j0, j1) in enumerate(() if away else WHOLE if len(cuts) > 2 else ((0, 8),)):
            step(e, b, "y%d%d" % (z, h), 0.001 * h)
            src = PB[p][:, 128 * j0:128 * j1]
            tt(src, src, T.nb[:, col + 128 * j0:col + 128 * j1], ALU.mult, banks(j0, j1) + names("nb", c, 0, 2), banks(j0, j1))
        for h, (j0, j1) in enumerate(runs):
            step(e, b, "d%d%d" % (z, min(h, 1)), 0.002 * h)
            tt(T.dd[:, 1024 * d + 128 * j0:1024 * d + 128 * j1], PB[p][:, 128 * j0:128 * j1],
               T.uu[:, col + 128 * j0:col + 128 * j1], ALU.add, names("u", c, j0 // 4, (j1 + 3) // 4) + banks(j0, j1),
               names("d", d, j0, j1))

        def sums(buf, c0, x, i, j0, j1, name):
            step(e, b, name)
            act(buf[:, c0 + 128 * j0:c0 + 128 * j1], buf[:, c0 + 128 * j0:c0 + 128 * j1], ACT.Abs, names(x, i, j0, j1),
                names(x, i, j0, j1))
            step(e, b, "m" + name.lstrip("a"))
            for j in range(j0, j1):
                total(buf, c0 + 128 * j, "%s%d%d" % (x, i, j), c, j)
        for h, (j0, j1) in enumerate(WHOLE if len(runs) == 1 else runs):
            sums(T.dd, 1024 * d, "d", d, j0, j1, "a%d%d" % (z, min(h, 1)))

        def held():
            for h, (j0, j1) in enumerate(away):
                sums(T.yy, col, "y", c, j0, j1, "h%d" % h)
        return held

    def decide(k, b):
        i = 2 * k + b
        bank = "pg%d" % b
        gw = PG[b][:, 0:64]
        if k == 0:
            z = PG[b][:, 64:128]
            ts(T.ci[:, b, :], z, 1.0 / KK, None, ALU.mult, None, [bank], [key("ci", 0, b)])
            tt(T.g0[:, 2 + b, :], z, T.ee[:, b, :], ALU.mult, [bank, "ee0", "ee1"], [key("ez", 0, b)])
            tt(T.g0[:, 4 + b, :], T.ci[:, b, :], T.cf[:, b, :], ALU.mult, [key("ci", 0, b), "cf0", "cf1"], [key("cz", 0, b)])
            tt(T.g0[:, 4 + b, :], T.g0[:, 4 + b, :], T.g0[:, 2 + b, :], ALU.add, [key("ez", 0, b), key("cz", 0, b)], [key("cz", 0, b)])
            for h in range(2):
                tt(T.gm[:, 2 + b, 32 * h:32 * h + 32], T.g0[:, 4 + b, 0:32], T.g0[:, 4 + b, 32:64], ALU.add,
                   [key("cz", 0, b)], [key("gm%d" % h, 1, b)])
            return
        gk = [key("gm0", k, b), key("gm1", k, b)]
        w = wr(k + 1, b)
        up, dl = PG[b][:, 384:448], PG[b][:, 448:512]
        step(k, b, "up")
        if k == RO:
            gw = PG[b][:, 0:32]
            tt(up[:, 0:32], gw, T.gm[:, 4 + b, 0:32], ALU.is_gt, [bank] + gk, [key("up", k, b)])
            tt(T.res[:, b, 32:64], gw, T.gm[:, 4 + b, 0:32], ALU.max, [bank] + gk, [key("rg", 0, b)])
            tt(dl[:, 0:32], up[:, 0:32], T.wk[:, w + 2, :], ALU.mult, [bank, key("up", k, b), key("sh", k, b)], [key("dl", k, b)])
            tt(T.res[:, b, 0:32], T.mu[:, b, :], dl[:, 0:32], ALU.subtract, [bank, key("mu", 0, b), key("dl", k, b)], [key("rm", 0, b)])
            step(k, b, "lis")
            for ph in range(2):
                mm(PG[b][64 * ph:64 * ph + 64, 128:192], T.res[:, b, :], T.idf[:, 64 * ph:64 * ph + 64], True, True,
                   [key("rg", 0, b), key("rm", 0, b), "idf"], [bank], True)
            step(k, b, "off")
            cp(T.rs[:, b, :], PG[b][:, 128:192], [bank], [key("rs", 0, b)])
            for part in back[b]:
                send([(peers[j], e0, ne, T.rs[:, b, :], T.rld[:, 2 * j + b, :], "rarr%d" % (2 * j + b)) for j, e0, ne in part],
                     [key("rs", 0, b)], [key("gone", 0, b)], LANDS["res"] * (3 - 2 * b))
            return
        i1, w1 = i + 2, wr(k + 2, b)
        if k == 1:
            tt(up, gw, T.gm[:, i, :], ALU.is_gt, [bank] + gk, [key("up", k, b)])
        else:
            ts(up, gw, 0.0, None, ALU.is_gt, None, [bank], [key("up", k, b)])
        step(k, b, "dl")
        tt(dl, up, T.wk[:, w + 1:w + 3, :], ALU.mult, [bank, key("up", k, b), key("sh", k, b), key("w", k + 1, b)], [key("dl", k, b)])
        step(k, b, "st")
        tt(T.st[:, sr(k + 1, b, 0):sr(k + 1, b, 2), :], T.st[:, sr(k - 1, b, 2):sr(k, b, 2):2, :], dl, ALU.subtract,
           [bank, key("mb", k, b), key("hf", k - 1, b), key("dl", k, b)], [key("mb", k + 1, b)])
        step(k, b, "tau")
        tt(T.tau[:, i, :], dl[:, 32:64], T.sg[:, i, :], ALU.subtract, [bank, key("dl", k, b), key("sg", k, b)], [key("tau", k, b)])
        step(k, b, "dx")
        tt(T.wk[:, w1 + 3, :], T.st[:, sr(k + 1, b, 0), :], T.st[:, sr(k, b, 2), :], ALU.subtract,
           [key("mb", k + 1, b), key("hf", k, b)], [key("dx", k + 1, b)])
        step(k, b, "hf")
        half(k + 1, b)
        step(k, b, "qq")
        tt(T.qq[:, i, :], T.wk[:, w1 + 3, :], T.tau[:, i, :], ALU.mult, [key("dx", k + 1, b), key("tau", k, b)], [key("qq", k, b)])
        step(k, b, "gm")
        gn = [key("gm0", k + 1, b), key("gm1", k + 1, b)]
        if k == 1:
            tt(T.gm[:, i1, :], gw, T.gm[:, i, :], ALU.max, [bank] + gk, gn)
        else:
            act(T.rl[:, b, :], gw, ACT.Relu, [bank], ["rl%d" % b])
            step(k, b, "gadd")
            op("g", lambda: g.dma_start(T.gm[:, 4 + b, :], T.rl[:, b, :], accum_op=ALU.add), ["rl%d" % b] + gk, gn + gk,
               1000.0, "accg%d" % b, 16 * (k - 1), late=LANDS["add"] + LANDS["add+"] * 0.5)
        step(k, b, "sg")
        ts(T.sg[:, i1, :], T.qq[:, i, :], 0.0, 0.5, ALU.is_ge, ALU.subtract, [key("qq", k, b)], [key("sg", k + 1, b)])
        step(k, b, "sh")
        stepped(k + 1, b)
        step(k, b, "w")
        probe(k + 1, b)
        step(k, b, "trn")
        turn(k + 2, b)
        step(k, b, "lis")
        buf = PG[b][:, 128:256]
        mm(buf, T.idh[:], T.log[:, 128 * b:128 * b + 128], True, False, ["idh", "log"], [bank])
        listed(buf, bank, k + 2, b, False, True)
        step(k, b, "off")
        c = 256 * (k + 3) + 128 * b
        ts(T.off[:, c:c + 128], buf, 2 * C0, None, ALU.add, None, [bank], [key("off", k + 3, b)])
        step(k, b, "t2")
        turned(k + 2, b)
        if k + 1 == RO:
            ts(T.mu[:, b, :], T.st[:, sr(RO, b, 1), :], C0, None, ALU.add, None, [key("mb", RO, b)], [key("mu", 0, b)])

    n = 0
    for e in range(1, RO + 1):
        for b in range(2):
            held = []
            opened[b] = None
            if 1 < e < RO:
                opened[b] = [16]
                step(e, b, "ini")
                mm(PG[b][:, 0:64], T.ndf[:], T.gm[:, 4 + b, :], True, False, ["ndf", key("gm0", e, b), key("gm1", e, b)],
                   ["pg%d" % b], True)
            for c in (2 * b, 2 * b + 1):
                if e == 1:
                    ends(c)
                    first(n, c)
                    n += 1
                    if c % 2:
                        step(e, b, "fsum")
                        decide(0, b)
                held.append(gain(n, e, c, LAST if e == RO and c == 3 else RUNS[c % 2]))
                n += 1
            for sums in held:
                sums()
            decide(e, b)
    here[:] = [99.0, None, None]

    outs = (T.ym, T.yg)
    for b in range(2):
        for i, x in enumerate((0,) + peers):
            for ph in range(2):
                for t in range(2):
                    row, col, p0 = 32 * (r ^ x), 128 * b + 64 * ph, 64 * ph + 32 * t
                    src = T.rld[p0:p0 + 32, 2 * i - 2 + b, :] if x else T.rs[p0:p0 + 32, b, :]
                    dma("a" if b == 1 and ph == 1 else "s", outs[t][row:row + 32, col:col + 64], src,
                        [key("gone" if x else "rs", 0, b)], [], "outs", 512,
                        [("rarr%d" % (2 * i - 2 + b), gets[b][i - 1])] if x else ())

    if not ORDER:
        ORDER.extend(arrange(plan))
    for i in ORDER:
        emit(plan[i])
    wait("g", "sent", sent[0])
    for q in cnt:
        wait("g", "c" + q, cnt[q])
    for s in sorted(totals):
        wait("g", s, totals[s])
